import numpy as np
import ml_dtypes


def mxq(x, axis, fmt="e4m3"):
    dtype, down = {"e4m3": (ml_dtypes.float8_e4m3fn, 7), "e5m2": (ml_dtypes.float8_e5m2, 14)}[fmt]
    v = np.moveaxis(np.asarray(x, np.float32).astype(ml_dtypes.bfloat16).astype(np.float64), axis, -1)
    blocks = v.reshape(v.shape[:-1] + (-1, 32))
    amax = np.abs(blocks).max(-1, keepdims=True)
    byte = np.maximum(np.where(amax > 0, np.frexp(amax)[1] - 1 + 127, 0) - down, 1)
    scale = np.exp2(byte - 127.0)
    codes = (blocks / scale).astype(np.float32).astype(dtype).astype(np.float64)
    return np.moveaxis((codes * scale).reshape(v.shape), -1, axis)


WIDE = False


def mx_kscale(k):
    if not WIDE:
        return np.ones(k)
    levels = np.array([18, -18])
    if k % 512:
        return np.exp2(np.random.permutation(np.resize(levels, k // 32))).repeat(32)
    a = np.empty((k // 512, 16))
    for p in range(k // 512):
        a[p, :8] = np.random.permutation(np.resize(levels, 8))
        for g in range(8):
            far = levels[np.abs(levels - a[p, g]) >= 10]
            a[p, g + 8] = far[np.random.randint(len(far))]
    return np.exp2(a.ravel()).repeat(32)


def f64(x):
    return np.asarray(x).astype(np.float64)


def striped(idx):
    return np.tile(np.asarray(idx).reshape(-1, 16).T, (8, 1)).astype(np.uint16)


def unstriped(offs):
    return offs[:16].T.reshape(-1).astype(np.int64)

def planes(y):
    n, m = y.shape
    v = y.astype(np.float32).astype(ml_dtypes.bfloat16).astype(np.float64).reshape(n // 32, 32, m)
    top = np.abs(v).max(1)
    byte = np.clip(np.where(top > 0, np.frexp(top)[1] - 1 + 127 - 7, 1), 1, 254)
    codes = (v * np.exp2(127.0 - byte)[:, None, :]).reshape(n, m).astype(np.float32).astype(ml_dtypes.float8_e4m3fn).view(np.uint8)
    words = codes.reshape(n // 512, 128, 4, m).transpose(0, 1, 3, 2)
    return np.ascontiguousarray(words), np.ascontiguousarray(byte.astype(np.uint8).reshape(n // 512, 16, m))


def setup_inputs():
    n = np.random.standard_normal
    uni = np.random.uniform
    idx = np.random.permutation(2048)[:512]
    jdx = np.random.permutation(1024)[:512]
    f_f = mx_kscale(512)
    return {
        "bT": (n((512, 1024))).astype(np.float32),
        "W": (n((512, 512)) / np.sqrt(512) * f_f[:, None]).astype(np.float32),
        "dz": (n((512, 512)) / f_f[:, None]).astype(np.float32),
        "offs": striped(idx),
        "joffs": striped(jdx),
    }


def reference(bT, W, dz, offs, joffs):
    idx = unstriped(offs)
    jdx = unstriped(joffs)
    b_ = f64(bT)[:, jdx]
    de = mxq(f64(W), 0, "e4m3").T @ mxq(f64(dz), 0, "e5m2")
    da = de * b_
    out_0 = np.zeros((512, 2048))
    out_0[:, idx] = da
    return (out_0,) + planes(out_0)

@@ -1,0 +1,174 @@
+from contextlib import ExitStack
+
+import concourse.mybir as mybir
+
+F32 = mybir.dt.float32
+BF16 = mybir.dt.bfloat16
+I32 = mybir.dt.int32
+U32 = mybir.dt.uint32
+U16 = mybir.dt.uint16
+U8 = mybir.dt.uint8
+E4M3X4 = mybir.dt.float8_e4m3fn_x4
+E5M2X4 = mybir.dt.float8_e5m2_x4
+MULT = mybir.AluOpType.mult
+
+P = 128
+LANES = 4
+D, F, ITEMS = 512, 512, 512
+A_COLS, B_COLS = 2048, 1024
+FLOPS = 2 * D * F * ITEMS
+
+PIECES = [(0, 512, "v"), (512, 256, "s"), (768, 256, "s"), (1024, 512, "v"), (1536, 256, "s"), (1792, 256, "s")]
+
+
+def tile_attend_gqr_a_pl_kernel(tc, bT, W, dz, offs, joffs, out_0, out_1, out_2):
+    nc = tc.nc
+    with ExitStack() as ctx:
+        lists = ctx.enter_context(tc.tile_pool(name="lists", bufs=1))
+        sb = ctx.enter_context(tc.tile_pool(name="sb", bufs=1))
+        psum = ctx.enter_context(tc.psum_pool(name="psum", bufs=1))
+
+        a_list = lists.tile([P, ITEMS // 16], U16, name="a_list")
+        b_list = lists.tile([P, ITEMS // 16], U16, name="b_list")
+
+        w_rows = W.rearrange("(p j) d -> p j d", j=LANES)
+        dz_rows = dz.rearrange("(p j) i -> p j i", j=LANES)
+        b_rows = bT.rearrange("(p t) c -> p t c", t=LANES)
+        out_rows = out_0.rearrange("(p t) c -> p t c", t=LANES)
+        words_out = out_1[0].rearrange("p c l -> p (c l)").bitcast(I32)
+        scales_out = out_2[0].bitcast(I32)
+
+        w_raw = [sb.tile([P, LANES, D // 2], F32, name=f"w_raw{h}") for h in range(2)]
+        dz_raw = [sb.tile([P, LANES, ITEMS // 2], F32, name=f"dz_raw{h}") for h in range(2)]
+        b_table = [sb.tile([P, B_COLS], F32, name=f"b_table{t}") for t in range(LANES)]
+        for h in range(2):
+            nc.sync.dma_start(w_raw[h][:], w_rows[:, :, h * 256 : (h + 1) * 256])
+        for h in range(2):
+            nc.sync.dma_start(dz_raw[h][:], dz_rows[:, :, h * 256 : (h + 1) * 256])
+        nc.sync.dma_start(b_list[:], joffs)
+        nc.sync.dma_start(a_list[:], offs)
+        for t in range(LANES):
+            nc.sync.dma_start(b_table[t][:], b_rows[:, t, :])
+
+        window = [sb.tile([P, A_COLS], F32, name=f"window{t}") for t in range(LANES)]
+        for t in range(LANES):
+            nc.vector.memset(window[t][:].bitcast(I32), 0)
+
+        w_bf = sb.tile([P, LANES, P, LANES], BF16, name="w_bf", align_bytes=64)
+        w_codes = sb.tile([P, D], U32, name="w_codes", align_bytes=64)
+        w_scales = sb.tile([P, D], U8, name="w_scales", align_bytes=64)
+        dz_bf = [sb.tile([P, ITEMS // 2, LANES], BF16, name=f"dz_bf{h}", align_bytes=64) for h in range(2)]
+        dz_codes = sb.tile([P, ITEMS], U32, name="dz_codes", align_bytes=64)
+        dz_scales = sb.tile([P, ITEMS], U8, name="dz_scales", align_bytes=64)
+
+        for h in range(2):
+            nc.scalar.copy(
+                w_bf[:, :, h * 64 : (h + 1) * 64, :].rearrange("p t m j -> p m t j"),
+                w_raw[h][:].rearrange("p j (m t) -> p m t j", t=LANES),
+            )
+
+        def cast_dz(h):
+            nc.vector.tensor_copy(dz_bf[h][:], dz_raw[h][:].rearrange("p j i -> p i j"))
+
+        def quantize_dz(h):
+            cols = slice(h * 256, (h + 1) * 256)
+            nc.vector.quantize_mx(
+                out=dz_codes[:, cols].bitcast(E5M2X4),
+                scales=dz_scales[:, cols],
+                in_=dz_bf[h][:].rearrange("p i j -> p (i j)"),
+            )
+
+        cast_dz(0)
+        nc.vector.quantize_mx(
+            out=w_codes[:].bitcast(E4M3X4),
+            scales=w_scales[:],
+            in_=w_bf[:].rearrange("p t m j -> p (t m j)"),
+        )
+        quantize_dz(0)
+        cast_dz(1)
+        quantize_dz(1)
+
+        de = []
+        for t in range(LANES):
+            bank = psum.tile([P, ITEMS], F32, name=f"bank{t}")
+            cols = slice(t * P, (t + 1) * P)
+            nc.tensor.matmul_mx(
+                out=bank[:],
+                lhsT=w_codes[:, cols].bitcast(E4M3X4),
+                lhsT_scale=w_scales[:, cols],
+                rhs=dz_codes[:].bitcast(E5M2X4),
+                rhs_scale=dz_scales[:],
+                start=True,
+                stop=True,
+            )
+            de_t = sb.tile([P, ITEMS], F32, name=f"de{t}")
+            nc.scalar.copy(de_t[:], bank[:])
+            de.append(de_t)
+
+        picked = [sb.tile([P, ITEMS], F32, name=f"picked{t}") for t in range(LANES)]
+        pairs = [sb.tile([P, 2, w, 2], BF16, name=f"pairs{k}", align_bytes=64) for k, (c0, w, e) in enumerate(PIECES)]
+
+        def gather(t):
+            nc.vector.tensor_copy(picked[t][:], b_table[t][:].indirect(b_list[:]))
+
+        def round_into_pairs(t, k, eng):
+            c0, w, e = PIECES[k]
+            dst = pairs[k][:, t // 2, :, t % 2]
+            if eng == "v":
+                nc.vector.tensor_copy(dst, window[t][:, c0 : c0 + w])
+            elif t == 2 and e == "v":
+                nc.scalar.copy(pairs[k][:, 1, :, :], window[t][:, c0 : c0 + w].unsqueeze(2).to_broadcast([P, w, 2]))
+            else:
+                nc.scalar.copy(dst, window[t][:, c0 : c0 + w])
+
+        def scatter(t):
+            nc.vector.tensor_tensor(window[t][:].indirect(a_list[:]), de[t][:], picked[t][:], MULT)
+            nc.sync.dma_start(out_rows[:, t, :], window[t][:])
+            if t < LANES - 1:
+                for k in range(len(PIECES)):
+                    round_into_pairs(t, k, "s")
+
+        gather(0)
+        gather(1)
+        scatter(0)
+        gather(2)
+        scatter(1)
+        scatter(2)
+        gather(3)
+        scatter(3)
+
+        y_bf = [sb.tile([P, w * LANES], BF16, name=f"y_bf{k}", align_bytes=64) for k, (c0, w, e) in enumerate(PIECES)]
+        y_codes = [sb.tile([P, w], U32, name=f"y_codes{k}", align_bytes=64) for k, (c0, w, e) in enumerate(PIECES)]
+        y_scales = sb.tile([P, A_COLS], U8, name="y_scales", align_bytes=64)
+
+        def weave(k):
+            c0, w, e = PIECES[k]
+            dt = I32 if e == "v" else U32
+            dst = y_bf[k][:].bitcast(dt).rearrange("p (c u) -> p c u", u=2)
+            src = pairs[k][:].rearrange("p u c e -> p u (c e)").bitcast(dt).rearrange("p u c -> p c u")
+            if e == "v":
+                nc.vector.tensor_copy(dst, src)
+            else:
+                nc.scalar.copy(dst, src)
+
+        def quantize_y(k):
+            c0, w, e = PIECES[k]
+            nc.vector.quantize_mx(
+                out=y_codes[k][:].bitcast(E4M3X4),
+                scales=y_scales[:, c0 : c0 + w],
+                in_=y_bf[k][:],
+            )
+            nc.sync.dma_start(words_out[:, c0 : c0 + w], y_codes[k][:].bitcast(I32))
+
+        for k in (1, 2, 4, 5):
+            round_into_pairs(3, k, "s")
+            weave(k)
+        round_into_pairs(3, 0, "v")
+        round_into_pairs(3, 3, "v")
+        weave(0)
+        weave(3)
+        for k in (0, 1, 2, 4, 3, 5):
+            quantize_y(k)
+        for q in range(4):
+            eng = nc.sync if q % 2 == 0 else nc.scalar
+            eng.dma_start(scales_out[4 * q : 4 * q + 4, :], y_scales[32 * q : 32 * q + 4, :].bitcast(I32))

@@ -18,7 +18,8 @@ D, F, ITEMS = 512, 512, 512
 A_COLS, B_COLS = 2048, 1024
 FLOPS = 2 * D * F * ITEMS
 
-PIECES = [(0, 512, "v"), (512, 256, "s"), (768, 256, "s"), (1024, 512, "v"), (1536, 256, "s"), (1792, 256, "s")]
+V_COLS = 1280
+PIECES = [(0, 512), (512, 512), (1024, 256), (1280, 256), (1536, 256), (1792, 256)]
 
 
 def tile_attend_gqr_a_pl_kernel(tc, bT, W, dz, offs, joffs, out_0, out_1, out_2):
@@ -46,9 +47,11 @@ def tile_attend_gqr_a_pl_kernel(tc, bT, W, dz, offs, joffs, out_0, out_1, out_2)
         for h in range(2):
             nc.sync.dma_start(dz_raw[h][:], dz_rows[:, :, h * 256 : (h + 1) * 256])
         nc.sync.dma_start(b_list[:], joffs)
+        nc.sync.dma_start(b_table[0][:], b_rows[:, 0, :])
+        nc.sync.dma_start(b_table[1][:], b_rows[:, 1, :])
         nc.sync.dma_start(a_list[:], offs)
-        for t in range(LANES):
-            nc.sync.dma_start(b_table[t][:], b_rows[:, t, :])
+        nc.sync.dma_start(b_table[2][:], b_rows[:, 2, :])
+        nc.sync.dma_start(b_table[3][:], b_rows[:, 3, :])
 
         window = [sb.tile([P, A_COLS], F32, name=f"window{t}") for t in range(LANES)]
         for t in range(LANES):
@@ -67,8 +70,8 @@ def tile_attend_gqr_a_pl_kernel(tc, bT, W, dz, offs, joffs, out_0, out_1, out_2)
                 w_raw[h][:].rearrange("p j (m t) -> p m t j", t=LANES),
             )
 
-        def cast_dz(h):
-            nc.vector.tensor_copy(dz_bf[h][:], dz_raw[h][:].rearrange("p j i -> p i j"))
+        def cast_dz(move, h, cols):
+            move(dz_bf[h][:, cols, :], dz_raw[h][:, :, cols].rearrange("p j i -> p i j"))
 
         def quantize_dz(h):
             cols = slice(h * 256, (h + 1) * 256)
@@ -78,14 +81,15 @@ def tile_attend_gqr_a_pl_kernel(tc, bT, W, dz, offs, joffs, out_0, out_1, out_2)
                 in_=dz_bf[h][:].rearrange("p i j -> p (i j)"),
             )
 
-        cast_dz(0)
+        cast_dz(nc.vector.tensor_copy, 0, slice(0, 256))
         nc.vector.quantize_mx(
             out=w_codes[:].bitcast(E4M3X4),
             scales=w_scales[:],
             in_=w_bf[:].rearrange("p t m j -> p (t m j)"),
         )
+        cast_dz(nc.vector.tensor_copy, 1, slice(0, 128))
+        cast_dz(nc.scalar.copy, 1, slice(128, 256))
         quantize_dz(0)
-        cast_dz(1)
         quantize_dz(1)
 
         de = []
@@ -105,54 +109,54 @@ def tile_attend_gqr_a_pl_kernel(tc, bT, W, dz, offs, joffs, out_0, out_1, out_2)
             nc.scalar.copy(de_t[:], bank[:])
             de.append(de_t)
 
-        picked = [sb.tile([P, ITEMS], F32, name=f"picked{t}") for t in range(LANES)]
-        pairs = [sb.tile([P, 2, w, 2], BF16, name=f"pairs{k}", align_bytes=64) for k, (c0, w, e) in enumerate(PIECES)]
+        shares = [(0, V_COLS), (V_COLS, A_COLS - V_COLS)]
+        pairs = [sb.tile([P, 2, n, 2], BF16, name=f"pairs{k}", align_bytes=64) for k, (c0, n) in enumerate(shares)]
+        picked = {}
 
         def gather(t):
+            picked[t] = sb.tile([P, ITEMS], F32, name=f"picked{t}", tag=f"picked{t % 2}")
             nc.vector.tensor_copy(picked[t][:], b_table[t][:].indirect(b_list[:]))
 
-        def round_into_pairs(t, k, eng):
-            c0, w, e = PIECES[k]
-            dst = pairs[k][:, t // 2, :, t % 2]
-            if eng == "v":
-                nc.vector.tensor_copy(dst, window[t][:, c0 : c0 + w])
-            elif t == 2 and e == "v":
-                nc.scalar.copy(pairs[k][:, 1, :, :], window[t][:, c0 : c0 + w].unsqueeze(2).to_broadcast([P, w, 2]))
-            else:
-                nc.scalar.copy(dst, window[t][:, c0 : c0 + w])
+        def round_into_pairs(move, t, share):
+            c0, n = shares[share]
+            move(pairs[share][:, t // 2, :, t % 2], window[t][:, c0 : c0 + n])
 
         def scatter(t):
             nc.vector.tensor_tensor(window[t][:].indirect(a_list[:]), de[t][:], picked[t][:], MULT)
             nc.sync.dma_start(out_rows[:, t, :], window[t][:])
-            if t < LANES - 1:
-                for k in range(len(PIECES)):
-                    round_into_pairs(t, k, "s")
+            if t < 2:
+                round_into_pairs(nc.scalar.copy, t, 0)
+            if t == 2:
+                both = window[t][:, :V_COLS].unsqueeze(2).to_broadcast([P, V_COLS, 2])
+                nc.scalar.copy(pairs[0][:, 1, :, :], both)
+            if t < 3:
+                round_into_pairs(nc.scalar.copy, t, 1)
 
         gather(0)
         gather(1)
         scatter(0)
-        gather(2)
         scatter(1)
-        scatter(2)
+        gather(2)
         gather(3)
+        scatter(2)
         scatter(3)
 
-        y_bf = [sb.tile([P, w * LANES], BF16, name=f"y_bf{k}", align_bytes=64) for k, (c0, w, e) in enumerate(PIECES)]
-        y_codes = [sb.tile([P, w], U32, name=f"y_codes{k}", align_bytes=64) for k, (c0, w, e) in enumerate(PIECES)]
+        y_bf = [sb.tile([P, w * LANES], BF16, name=f"y_bf{k}", align_bytes=64) for k, (c0, w) in enumerate(PIECES)]
+        y_codes = [sb.tile([P, w], U32, name=f"y_codes{k}", align_bytes=64) for k, (c0, w) in enumerate(PIECES)]
         y_scales = sb.tile([P, A_COLS], U8, name="y_scales", align_bytes=64)
 
-        def weave(k):
-            c0, w, e = PIECES[k]
-            dt = I32 if e == "v" else U32
-            dst = y_bf[k][:].bitcast(dt).rearrange("p (c u) -> p c u", u=2)
-            src = pairs[k][:].rearrange("p u c e -> p u (c e)").bitcast(dt).rearrange("p u c -> p c u")
-            if e == "v":
-                nc.vector.tensor_copy(dst, src)
-            else:
-                nc.scalar.copy(dst, src)
+        def weave(move, word, k):
+            c0, w = PIECES[k]
+            share = 0 if c0 < V_COLS else 1
+            c0 -= shares[share][0]
+            words = pairs[share][:].rearrange("p u c e -> p u (c e)").bitcast(word)
+            move(
+                y_bf[k][:].bitcast(word).rearrange("p (c u) -> p c u", u=2),
+                words[:, :, c0 : c0 + w].rearrange("p u c -> p c u"),
+            )
 
         def quantize_y(k):
-            c0, w, e = PIECES[k]
+            c0, w = PIECES[k]
             nc.vector.quantize_mx(
                 out=y_codes[k][:].bitcast(E4M3X4),
                 scales=y_scales[:, c0 : c0 + w],
@@ -160,14 +164,13 @@ def tile_attend_gqr_a_pl_kernel(tc, bT, W, dz, offs, joffs, out_0, out_1, out_2)
             )
             nc.sync.dma_start(words_out[:, c0 : c0 + w], y_codes[k][:].bitcast(I32))
 
-        for k in (1, 2, 4, 5):
-            round_into_pairs(3, k, "s")
-            weave(k)
-        round_into_pairs(3, 0, "v")
-        round_into_pairs(3, 3, "v")
-        weave(0)
-        weave(3)
-        for k in (0, 1, 2, 4, 3, 5):
+        round_into_pairs(nc.scalar.copy, 3, 1)
+        for k in (3, 4, 5):
+            weave(nc.scalar.copy, U32, k)
+        round_into_pairs(nc.vector.tensor_copy, 3, 0)
+        for k in (0, 1, 2):
+            weave(nc.vector.tensor_copy, I32, k)
+        for k in range(len(PIECES)):
             quantize_y(k)
         for q in range(4):
             eng = nc.sync if q % 2 == 0 else nc.scalar

@@ -18,8 +18,14 @@ D, F, ITEMS = 512, 512, 512
 A_COLS, B_COLS = 2048, 1024
 FLOPS = 2 * D * F * ITEMS
 
-V_COLS = 1280
-PIECES = [(0, 512), (512, 512), (1024, 256), (1280, 256), (1536, 256), (1792, 256)]
+V_COLS = 960
+V_BOTH = 256
+STRIP = 512
+ORDER_COLS = 8
+PIECES = [(c0, 256) for c0 in range(0, A_COLS, 256)]
+CODE_STORES = [(0, 512), (512, 512), (1024, 512), (1536, 256), (1792, 256)]
+V_WEAVES = [(256, 256), (0, 256), (512, 256), (768, 192)]
+S_WEAVES = [(960, 64), (1024, 256), (1280, 256), (1536, 256), (1792, 256)]
 
 
 def tile_attend_gqr_a_pl_kernel(tc, bT, W, dz, offs, joffs, out_0, out_1, out_2):
@@ -39,17 +45,16 @@ def tile_attend_gqr_a_pl_kernel(tc, bT, W, dz, offs, joffs, out_0, out_1, out_2)
         words_out = out_1[0].rearrange("p c l -> p (c l)").bitcast(I32)
         scales_out = out_2[0].bitcast(I32)
 
-        w_raw = [sb.tile([P, LANES, D // 2], F32, name=f"w_raw{h}") for h in range(2)]
-        dz_raw = [sb.tile([P, LANES, ITEMS // 2], F32, name=f"dz_raw{h}") for h in range(2)]
+        w_raw = [sb.tile([P, 2, D], F32, name=f"w_raw{v}") for v in range(2)]
+        dz_raw = sb.tile([P, LANES, ITEMS], F32, name="dz_raw")
         b_table = [sb.tile([P, B_COLS], F32, name=f"b_table{t}") for t in range(LANES)]
-        for h in range(2):
-            nc.sync.dma_start(w_raw[h][:], w_rows[:, :, h * 256 : (h + 1) * 256])
-        for h in range(2):
-            nc.sync.dma_start(dz_raw[h][:], dz_rows[:, :, h * 256 : (h + 1) * 256])
+        nc.sync.dma_start(dz_raw[:], dz_rows)
+        for v in range(2):
+            nc.sync.dma_start(w_raw[v][:], w_rows[:, 2 * v : 2 * v + 2, :])
         nc.sync.dma_start(b_list[:], joffs)
         nc.sync.dma_start(b_table[0][:], b_rows[:, 0, :])
-        nc.sync.dma_start(b_table[1][:], b_rows[:, 1, :])
         nc.sync.dma_start(a_list[:], offs)
+        nc.sync.dma_start(b_table[1][:], b_rows[:, 1, :])
         nc.sync.dma_start(b_table[2][:], b_rows[:, 2, :])
         nc.sync.dma_start(b_table[3][:], b_rows[:, 3, :])
 
@@ -57,21 +62,17 @@ def tile_attend_gqr_a_pl_kernel(tc, bT, W, dz, offs, joffs, out_0, out_1, out_2)
         for t in range(LANES):
             nc.vector.memset(window[t][:].bitcast(I32), 0)
 
-        w_bf = sb.tile([P, LANES, P, LANES], BF16, name="w_bf", align_bytes=64)
-        w_codes = sb.tile([P, D], U32, name="w_codes", align_bytes=64)
-        w_scales = sb.tile([P, D], U8, name="w_scales", align_bytes=64)
-        dz_bf = [sb.tile([P, ITEMS // 2, LANES], BF16, name=f"dz_bf{h}", align_bytes=64) for h in range(2)]
-        dz_codes = sb.tile([P, ITEMS], U32, name="dz_codes", align_bytes=64)
+        w_bf = [sb.tile([P, 2, P, LANES], BF16, name=f"w_bf{u}", align_bytes=64) for u in range(2)]
+        w_codes = [sb.tile([P, 2 * P], U32, name=f"w_codes{u}", tag=["w_codes0", "slot1"][u], align_bytes=64) for u in range(2)]
+        w_scales = [sb.tile([P, 2 * P], U8, name=f"w_scales{u}", align_bytes=64) for u in range(2)]
+        dz_bf = [sb.tile([P, ITEMS // 2, LANES], BF16, name=f"dz_bf{h}", tag=["dz_bf0", "slot0"][h], align_bytes=64) for h in range(2)]
+        dz_codes = sb.tile([P, ITEMS], U32, name="dz_codes", tag="slot2", align_bytes=64)
         dz_scales = sb.tile([P, ITEMS], U8, name="dz_scales", align_bytes=64)
+        picked = {}
+        de = {}
 
-        for h in range(2):
-            nc.scalar.copy(
-                w_bf[:, :, h * 64 : (h + 1) * 64, :].rearrange("p t m j -> p m t j"),
-                w_raw[h][:].rearrange("p j (m t) -> p m t j", t=LANES),
-            )
-
-        def cast_dz(move, h, cols):
-            move(dz_bf[h][:, cols, :], dz_raw[h][:, :, cols].rearrange("p j i -> p i j"))
+        def round_dz(move, h, i0, n):
+            move(dz_bf[h][:, i0 : i0 + n, :], dz_raw[:, :, h * 256 + i0 : h * 256 + i0 + n].rearrange("p j i -> p i j"))
 
         def quantize_dz(h):
             cols = slice(h * 256, (h + 1) * 256)
@@ -81,97 +82,130 @@ def tile_attend_gqr_a_pl_kernel(tc, bT, W, dz, offs, joffs, out_0, out_1, out_2)
                 in_=dz_bf[h][:].rearrange("p i j -> p (i j)"),
             )
 
-        cast_dz(nc.vector.tensor_copy, 0, slice(0, 256))
-        nc.vector.quantize_mx(
-            out=w_codes[:].bitcast(E4M3X4),
-            scales=w_scales[:],
-            in_=w_bf[:].rearrange("p t m j -> p (t m j)"),
-        )
-        cast_dz(nc.vector.tensor_copy, 1, slice(0, 128))
-        cast_dz(nc.scalar.copy, 1, slice(128, 256))
-        quantize_dz(0)
-        quantize_dz(1)
+        def round_w(move, u, v):
+            move(
+                w_bf[u][:, :, :, 2 * v : 2 * v + 2].rearrange("p t m j -> p m t j"),
+                w_raw[v][:].rearrange("p j (m t) -> p m t j", t=LANES)[:, :, 2 * u : 2 * u + 2, :],
+            )
 
-        de = []
-        for t in range(LANES):
+        def quantize_w(u):
+            nc.vector.quantize_mx(
+                out=w_codes[u][:].bitcast(E4M3X4),
+                scales=w_scales[u][:],
+                in_=w_bf[u][:].rearrange("p t m j -> p (t m j)"),
+            )
+
+        def product(t):
             bank = psum.tile([P, ITEMS], F32, name=f"bank{t}")
-            cols = slice(t * P, (t + 1) * P)
+            cols = slice((t % 2) * P, (t % 2 + 1) * P)
             nc.tensor.matmul_mx(
                 out=bank[:],
-                lhsT=w_codes[:, cols].bitcast(E4M3X4),
-                lhsT_scale=w_scales[:, cols],
+                lhsT=w_codes[t // 2][:, cols].bitcast(E4M3X4),
+                lhsT_scale=w_scales[t // 2][:, cols],
                 rhs=dz_codes[:].bitcast(E5M2X4),
                 rhs_scale=dz_scales[:],
                 start=True,
                 stop=True,
             )
-            de_t = sb.tile([P, ITEMS], F32, name=f"de{t}")
-            nc.scalar.copy(de_t[:], bank[:])
-            de.append(de_t)
-
-        shares = [(0, V_COLS), (V_COLS, A_COLS - V_COLS)]
-        pairs = [sb.tile([P, 2, n, 2], BF16, name=f"pairs{k}", align_bytes=64) for k, (c0, n) in enumerate(shares)]
-        picked = {}
+            de[t] = sb.tile([P, ITEMS], F32, name=f"de{t}")
+            nc.scalar.copy(de[t][:], bank[:])
 
         def gather(t):
-            picked[t] = sb.tile([P, ITEMS], F32, name=f"picked{t}", tag=f"picked{t % 2}")
+            picked[t] = sb.tile([P, ITEMS], F32, name=f"picked{t}", tag=f"slot{t % 3}", align_bytes=64)
             nc.vector.tensor_copy(picked[t][:], b_table[t][:].indirect(b_list[:]))
 
-        def round_into_pairs(move, t, share):
-            c0, n = shares[share]
-            move(pairs[share][:, t // 2, :, t % 2], window[t][:, c0 : c0 + n])
+        shares = [(0, V_BOTH), (V_BOTH, V_COLS - V_BOTH), (V_COLS, A_COLS - V_COLS)]
+        pairs = [sb.tile([P, 2, n, 2], BF16, name=f"pairs{k}", align_bytes=64) for k, (c0, n) in enumerate(shares)]
+
+        def share_of(c):
+            return max(i for i, (s, n) in enumerate(shares) if s <= c)
+
+        def round_into_pairs(move, t, c0, c1):
+            share = share_of(c0)
+            base = shares[share][0]
+            move(pairs[share][:, t // 2, c0 - base : c1 - base, t % 2], window[t][:, c0:c1])
 
         def scatter(t):
             nc.vector.tensor_tensor(window[t][:].indirect(a_list[:]), de[t][:], picked[t][:], MULT)
             nc.sync.dma_start(out_rows[:, t, :], window[t][:])
             if t < 2:
-                round_into_pairs(nc.scalar.copy, t, 0)
+                round_into_pairs(nc.scalar.copy, t, 0, V_BOTH)
+                round_into_pairs(nc.scalar.copy, t, V_BOTH, V_COLS)
             if t == 2:
-                both = window[t][:, :V_COLS].unsqueeze(2).to_broadcast([P, V_COLS, 2])
-                nc.scalar.copy(pairs[0][:, 1, :, :], both)
+                n = V_COLS - ORDER_COLS
+                round_into_pairs(nc.scalar.copy, t, V_BOTH, n)
+                both = window[t][:, n:V_COLS].unsqueeze(2).to_broadcast([P, ORDER_COLS, 2])
+                nc.scalar.copy(pairs[1][:, 1, n - V_BOTH :, :], both)
             if t < 3:
-                round_into_pairs(nc.scalar.copy, t, 1)
+                round_into_pairs(nc.scalar.copy, t, V_COLS, A_COLS)
 
+        round_dz(nc.scalar.copy, 0, 0, 256)
+        round_dz(nc.scalar.copy, 1, 0, 128)
+        round_w(nc.vector.tensor_copy, 0, 0)
+        round_dz(nc.vector.tensor_copy, 1, 128, 128)
+        round_w(nc.scalar.copy, 1, 0)
+        quantize_dz(0)
+        round_w(nc.vector.tensor_copy, 0, 1)
+        round_w(nc.scalar.copy, 1, 1)
+        quantize_dz(1)
+        quantize_w(0)
+        product(0)
+        product(1)
         gather(0)
-        gather(1)
+        quantize_w(1)
+        product(2)
+        product(3)
         scatter(0)
-        scatter(1)
+        gather(1)
         gather(2)
+        scatter(1)
         gather(3)
         scatter(2)
         scatter(3)
 
         y_bf = [sb.tile([P, w * LANES], BF16, name=f"y_bf{k}", align_bytes=64) for k, (c0, w) in enumerate(PIECES)]
-        y_codes = [sb.tile([P, w], U32, name=f"y_codes{k}", align_bytes=64) for k, (c0, w) in enumerate(PIECES)]
-        y_scales = sb.tile([P, A_COLS], U8, name="y_scales", align_bytes=64)
+        y_codes = sb.tile([P, A_COLS], U32, name="y_codes", align_bytes=64)
+        y_scales = sb.tile([P, STRIP], U8, name="y_scales", align_bytes=64)
 
-        def weave(move, word, k):
-            c0, w = PIECES[k]
-            share = 0 if c0 < V_COLS else 1
+        def weave(move, word, c0, w):
+            k = max(i for i, (s, n) in enumerate(PIECES) if s <= c0)
+            y0 = c0 - PIECES[k][0]
+            share = share_of(c0)
             c0 -= shares[share][0]
             words = pairs[share][:].rearrange("p u c e -> p u (c e)").bitcast(word)
             move(
-                y_bf[k][:].bitcast(word).rearrange("p (c u) -> p c u", u=2),
+                y_bf[k][:].bitcast(word).rearrange("p (c u) -> p c u", u=2)[:, y0 : y0 + w, :],
                 words[:, :, c0 : c0 + w].rearrange("p u c -> p c u"),
             )
 
         def quantize_y(k):
-            c0, w = PIECES[k]
+            c0, n = PIECES[k]
+            strip, s0 = divmod(c0, STRIP)
             nc.vector.quantize_mx(
-                out=y_codes[k][:].bitcast(E4M3X4),
-                scales=y_scales[:, c0 : c0 + w],
+                out=y_codes[:, c0 : c0 + n].bitcast(E4M3X4),
+                scales=y_scales[4 * strip :, s0 : s0 + n],
                 in_=y_bf[k][:],
             )
-            nc.sync.dma_start(words_out[:, c0 : c0 + w], y_codes[k][:].bitcast(I32))
+            for s, w in CODE_STORES:
+                if s + w == c0 + n:
+                    nc.sync.dma_start(words_out[:, s : s + w], y_codes[:, s : s + w].bitcast(I32))
 
-        round_into_pairs(nc.scalar.copy, 3, 1)
-        for k in (3, 4, 5):
-            weave(nc.scalar.copy, U32, k)
-        round_into_pairs(nc.vector.tensor_copy, 3, 0)
-        for k in (0, 1, 2):
-            weave(nc.vector.tensor_copy, I32, k)
-        for k in range(len(PIECES)):
+        round_into_pairs(nc.scalar.copy, 3, V_COLS, A_COLS)
+        for c0, w in S_WEAVES:
+            weave(nc.scalar.copy, U32, c0, w)
+        round_into_pairs(nc.vector.tensor_copy, 2, 0, V_BOTH)
+        round_into_pairs(nc.vector.tensor_copy, 3, V_BOTH, V_COLS)
+        round_into_pairs(nc.vector.tensor_copy, 3, 0, V_BOTH)
+        for c0, w in V_WEAVES[:3]:
+            weave(nc.vector.tensor_copy, I32, c0, w)
+        quantize_y(0)
+        quantize_y(1)
+        weave(nc.vector.tensor_copy, I32, *V_WEAVES[3])
+        for k in range(2, len(PIECES)):
             quantize_y(k)
         for q in range(4):
-            eng = nc.sync if q % 2 == 0 else nc.scalar
-            eng.dma_start(scales_out[4 * q : 4 * q + 4, :], y_scales[32 * q : 32 * q + 4, :].bitcast(I32))
+            eng = nc.scalar if q % 2 == 0 else nc.sync
+            eng.dma_start(
+                scales_out[4 * q : 4 * q + 4, :].rearrange("r (s c) -> s r c", s=4),
+                y_scales[32 * q : 32 * q + 16, :].bitcast(I32),
+            )

@@ -21,6 +21,7 @@ FLOPS = 2 * D * F * ITEMS
 V_COLS = 960
 V_BOTH = 256
 STRIP = 512
+W_GROUPS = [(0, 1), (1, 1), (2, 2)]
 ORDER_COLS = 8
 PIECES = [(c0, 256) for c0 in range(0, A_COLS, 256)]
 CODE_STORES = [(0, 512), (512, 512), (1024, 512), (1536, 256), (1792, 256)]
@@ -49,24 +50,25 @@ def tile_attend_gqr_a_pl_kernel(tc, bT, W, dz, offs, joffs, out_0, out_1, out_2)
         dz_raw = sb.tile([P, LANES, ITEMS], F32, name="dz_raw")
         b_table = [sb.tile([P, B_COLS], F32, name=f"b_table{t}") for t in range(LANES)]
         nc.sync.dma_start(dz_raw[:], dz_rows)
-        for v in range(2):
-            nc.sync.dma_start(w_raw[v][:], w_rows[:, 2 * v : 2 * v + 2, :])
         nc.sync.dma_start(b_list[:], joffs)
         nc.sync.dma_start(b_table[0][:], b_rows[:, 0, :])
-        nc.sync.dma_start(a_list[:], offs)
+        for v in range(2):
+            nc.sync.dma_start(w_raw[v][:], w_rows[:, 2 * v : 2 * v + 2, :])
         nc.sync.dma_start(b_table[1][:], b_rows[:, 1, :])
+        nc.sync.dma_start(a_list[:], offs)
         nc.sync.dma_start(b_table[2][:], b_rows[:, 2, :])
         nc.sync.dma_start(b_table[3][:], b_rows[:, 3, :])
 
-        window = [sb.tile([P, A_COLS], F32, name=f"window{t}") for t in range(LANES)]
-        for t in range(LANES):
-            nc.vector.memset(window[t][:].bitcast(I32), 0)
+        window = [sb.tile([P, A_COLS], F32, name=f"window{u}") for u in range(2)] * 2
+        for u in range(2):
+            nc.vector.memset(window[u][:].bitcast(I32), 0)
 
-        w_bf = [sb.tile([P, 2, P, LANES], BF16, name=f"w_bf{u}", align_bytes=64) for u in range(2)]
-        w_codes = [sb.tile([P, 2 * P], U32, name=f"w_codes{u}", tag=["w_codes0", "slot1"][u], align_bytes=64) for u in range(2)]
-        w_scales = [sb.tile([P, 2 * P], U8, name=f"w_scales{u}", align_bytes=64) for u in range(2)]
-        dz_bf = [sb.tile([P, ITEMS // 2, LANES], BF16, name=f"dz_bf{h}", tag=["dz_bf0", "slot0"][h], align_bytes=64) for h in range(2)]
-        dz_codes = sb.tile([P, ITEMS], U32, name="dz_codes", tag="slot2", align_bytes=64)
+        w_tags = ["w_bf0", "slot1", "w_bf2"]
+        w_bf = [sb.tile([P, n, P, LANES], BF16, name=f"w_bf{g}", tag=w_tags[g], align_bytes=64) for g, (t0, n) in enumerate(W_GROUPS)]
+        w_codes = [sb.tile([P, n * P], U32, name=f"w_codes{g}", align_bytes=64) for g, (t0, n) in enumerate(W_GROUPS)]
+        w_scales = [sb.tile([P, n * P], U8, name=f"w_scales{g}", align_bytes=64) for g, (t0, n) in enumerate(W_GROUPS)]
+        dz_bf = [sb.tile([P, ITEMS // 2, LANES], BF16, name=f"dz_bf{h}", align_bytes=64) for h in range(2)]
+        dz_codes = sb.tile([P, ITEMS], U32, name="dz_codes", align_bytes=64)
         dz_scales = sb.tile([P, ITEMS], U8, name="dz_scales", align_bytes=64)
         picked = {}
         de = {}
@@ -82,10 +84,11 @@ def tile_attend_gqr_a_pl_kernel(tc, bT, W, dz, offs, joffs, out_0, out_1, out_2)
                 in_=dz_bf[h][:].rearrange("p i j -> p (i j)"),
             )
 
-        def round_w(move, u, v):
+        def round_w(move, g, v):
+            t0, n = W_GROUPS[g]
             move(
-                w_bf[u][:, :, :, 2 * v : 2 * v + 2].rearrange("p t m j -> p m t j"),
-                w_raw[v][:].rearrange("p j (m t) -> p m t j", t=LANES)[:, :, 2 * u : 2 * u + 2, :],
+                w_bf[g][:, :, :, 2 * v : 2 * v + 2].rearrange("p t m j -> p m t j"),
+                w_raw[v][:].rearrange("p j (m t) -> p m t j", t=LANES)[:, :, t0 : t0 + n, :],
             )
 
         def quantize_w(u):
@@ -97,11 +100,12 @@ def tile_attend_gqr_a_pl_kernel(tc, bT, W, dz, offs, joffs, out_0, out_1, out_2)
 
         def product(t):
             bank = psum.tile([P, ITEMS], F32, name=f"bank{t}")
-            cols = slice((t % 2) * P, (t % 2 + 1) * P)
+            g = min(t, 2)
+            cols = slice((t - g) * P, (t - g + 1) * P)
             nc.tensor.matmul_mx(
                 out=bank[:],
-                lhsT=w_codes[t // 2][:, cols].bitcast(E4M3X4),
-                lhsT_scale=w_scales[t // 2][:, cols],
+                lhsT=w_codes[g][:, cols].bitcast(E4M3X4),
+                lhsT_scale=w_scales[g][:, cols],
                 rhs=dz_codes[:].bitcast(E5M2X4),
                 rhs_scale=dz_scales[:],
                 start=True,
@@ -111,7 +115,7 @@ def tile_attend_gqr_a_pl_kernel(tc, bT, W, dz, offs, joffs, out_0, out_1, out_2)
             nc.scalar.copy(de[t][:], bank[:])
 
         def gather(t):
-            picked[t] = sb.tile([P, ITEMS], F32, name=f"picked{t}", tag=f"slot{t % 3}", align_bytes=64)
+            picked[t] = sb.tile([P, ITEMS], F32, name=f"picked{t}", tag=f"slot{t % 2}", align_bytes=64)
             nc.vector.tensor_copy(picked[t][:], b_table[t][:].indirect(b_list[:]))
 
         shares = [(0, V_BOTH), (V_BOTH, V_COLS - V_BOTH), (V_COLS, A_COLS - V_COLS)]
@@ -140,25 +144,25 @@ def tile_attend_gqr_a_pl_kernel(tc, bT, W, dz, offs, joffs, out_0, out_1, out_2)
                 round_into_pairs(nc.scalar.copy, t, V_COLS, A_COLS)
 
         round_dz(nc.scalar.copy, 0, 0, 256)
-        round_dz(nc.scalar.copy, 1, 0, 128)
-        round_w(nc.vector.tensor_copy, 0, 0)
-        round_dz(nc.vector.tensor_copy, 1, 128, 128)
-        round_w(nc.scalar.copy, 1, 0)
-        quantize_dz(0)
-        round_w(nc.vector.tensor_copy, 0, 1)
-        round_w(nc.scalar.copy, 1, 1)
+        round_dz(nc.vector.tensor_copy, 1, 0, 256)
+        gather(0)
         quantize_dz(1)
+        quantize_dz(0)
+        for v in range(2):
+            round_w(nc.vector.tensor_copy, 0, v)
+            round_w(nc.vector.tensor_copy, 1, v)
+            round_w(nc.scalar.copy, 2, v)
         quantize_w(0)
         product(0)
-        product(1)
-        gather(0)
         quantize_w(1)
+        product(1)
+        quantize_w(2)
         product(2)
         product(3)
-        scatter(0)
         gather(1)
-        gather(2)
+        scatter(0)
         scatter(1)
+        gather(2)
         gather(3)
         scatter(2)
         scatter(3)

@@ -24,7 +24,7 @@ STRIP = 512
 W_GROUPS = [(0, 1), (1, 1), (2, 2)]
 ORDER_COLS = 8
 PIECES = [(c0, 256) for c0 in range(0, A_COLS, 256)]
-CODE_STORES = [(0, 512), (512, 512), (1024, 512), (1536, 256), (1792, 256)]
+CODE_STORES = [(0, 768), (768, 768), (1536, 512)]
 V_WEAVES = [(256, 256), (0, 256), (512, 256), (768, 192)]
 S_WEAVES = [(960, 64), (1024, 256), (1280, 256), (1536, 256), (1792, 256)]
 
@@ -59,9 +59,10 @@ def tile_attend_gqr_a_pl_kernel(tc, bT, W, dz, offs, joffs, out_0, out_1, out_2)
         nc.sync.dma_start(b_table[2][:], b_rows[:, 2, :])
         nc.sync.dma_start(b_table[3][:], b_rows[:, 3, :])
 
-        window = [sb.tile([P, A_COLS], F32, name=f"window{u}") for u in range(2)] * 2
-        for u in range(2):
+        window = [sb.tile([P, A_COLS], F32, name=f"window{u}") for u in range(3)]
+        for u in range(3):
             nc.vector.memset(window[u][:].bitcast(I32), 0)
+        window.append(window[0])
 
         w_tags = ["w_bf0", "slot1", "w_bf2"]
         w_bf = [sb.tile([P, n, P, LANES], BF16, name=f"w_bf{g}", tag=w_tags[g], align_bytes=64) for g, (t0, n) in enumerate(W_GROUPS)]

@@ -18,15 +18,15 @@ D, F, ITEMS = 512, 512, 512
 A_COLS, B_COLS = 2048, 1024
 FLOPS = 2 * D * F * ITEMS
 
-V_COLS = 960
-V_BOTH = 256
+V_COLS = 1024
+V_BOTH = 512
 STRIP = 512
-W_GROUPS = [(0, 1), (1, 1), (2, 2)]
+W_GROUPS = [(0, 2), (2, 2)]
 ORDER_COLS = 8
 PIECES = [(c0, 256) for c0 in range(0, A_COLS, 256)]
-CODE_STORES = [(0, 768), (768, 768), (1536, 512)]
-V_WEAVES = [(256, 256), (0, 256), (512, 256), (768, 192)]
-S_WEAVES = [(960, 64), (1024, 256), (1280, 256), (1536, 256), (1792, 256)]
+CODE_STORES = [(0, 512), (512, 512), (1024, 512), (1536, 256), (1792, 256)]
+V_WEAVES = [(512, 256), (0, 256), (256, 256), (768, 256)]
+S_WEAVES = [(1024, 256), (1280, 256), (1536, 256), (1792, 256)]
 
 
 def tile_attend_gqr_a_pl_kernel(tc, bT, W, dz, offs, joffs, out_0, out_1, out_2):
@@ -59,12 +59,11 @@ def tile_attend_gqr_a_pl_kernel(tc, bT, W, dz, offs, joffs, out_0, out_1, out_2)
         nc.sync.dma_start(b_table[2][:], b_rows[:, 2, :])
         nc.sync.dma_start(b_table[3][:], b_rows[:, 3, :])
 
-        window = [sb.tile([P, A_COLS], F32, name=f"window{u}") for u in range(3)]
-        for u in range(3):
+        window = [sb.tile([P, A_COLS], F32, name=f"window{u}") for u in range(2)] * 2
+        for u in range(2):
             nc.vector.memset(window[u][:].bitcast(I32), 0)
-        window.append(window[0])
 
-        w_tags = ["w_bf0", "slot1", "w_bf2"]
+        w_tags = ["slot1", "w_bf1"]
         w_bf = [sb.tile([P, n, P, LANES], BF16, name=f"w_bf{g}", tag=w_tags[g], align_bytes=64) for g, (t0, n) in enumerate(W_GROUPS)]
         w_codes = [sb.tile([P, n * P], U32, name=f"w_codes{g}", align_bytes=64) for g, (t0, n) in enumerate(W_GROUPS)]
         w_scales = [sb.tile([P, n * P], U8, name=f"w_scales{g}", align_bytes=64) for g, (t0, n) in enumerate(W_GROUPS)]
@@ -92,17 +91,17 @@ def tile_attend_gqr_a_pl_kernel(tc, bT, W, dz, offs, joffs, out_0, out_1, out_2)
                 w_raw[v][:].rearrange("p j (m t) -> p m t j", t=LANES)[:, :, t0 : t0 + n, :],
             )
 
-        def quantize_w(u):
+        def quantize_w(u, t0, n):
             nc.vector.quantize_mx(
-                out=w_codes[u][:].bitcast(E4M3X4),
-                scales=w_scales[u][:],
-                in_=w_bf[u][:].rearrange("p t m j -> p (t m j)"),
+                out=w_codes[u][:, t0 * P : (t0 + n) * P].bitcast(E4M3X4),
+                scales=w_scales[u][:, t0 * P : (t0 + n) * P],
+                in_=w_bf[u][:, t0 : t0 + n].rearrange("p t m j -> p (t m j)"),
             )
 
         def product(t):
             bank = psum.tile([P, ITEMS], F32, name=f"bank{t}")
-            g = min(t, 2)
-            cols = slice((t - g) * P, (t - g + 1) * P)
+            g = t // 2
+            cols = slice((t % 2) * P, (t % 2 + 1) * P)
             nc.tensor.matmul_mx(
                 out=bank[:],
                 lhsT=w_codes[g][:, cols].bitcast(E4M3X4),
@@ -119,7 +118,7 @@ def tile_attend_gqr_a_pl_kernel(tc, bT, W, dz, offs, joffs, out_0, out_1, out_2)
             picked[t] = sb.tile([P, ITEMS], F32, name=f"picked{t}", tag=f"slot{t % 2}", align_bytes=64)
             nc.vector.tensor_copy(picked[t][:], b_table[t][:].indirect(b_list[:]))
 
-        shares = [(0, V_BOTH), (V_BOTH, V_COLS - V_BOTH), (V_COLS, A_COLS - V_COLS)]
+        shares = [(c0, 512) for c0 in range(0, A_COLS, 512)]
         pairs = [sb.tile([P, 2, n, 2], BF16, name=f"pairs{k}", align_bytes=64) for k, (c0, n) in enumerate(shares)]
 
         def share_of(c):
@@ -137,12 +136,14 @@ def tile_attend_gqr_a_pl_kernel(tc, bT, W, dz, offs, joffs, out_0, out_1, out_2)
                 round_into_pairs(nc.scalar.copy, t, 0, V_BOTH)
                 round_into_pairs(nc.scalar.copy, t, V_BOTH, V_COLS)
             if t == 2:
-                n = V_COLS - ORDER_COLS
-                round_into_pairs(nc.scalar.copy, t, V_BOTH, n)
-                both = window[t][:, n:V_COLS].unsqueeze(2).to_broadcast([P, ORDER_COLS, 2])
-                nc.scalar.copy(pairs[1][:, 1, n - V_BOTH :, :], both)
-            if t < 3:
-                round_into_pairs(nc.scalar.copy, t, V_COLS, A_COLS)
+                for share in range(2):
+                    c0, n = shares[share]
+                    c1 = c0 + n - ORDER_COLS
+                    round_into_pairs(nc.scalar.copy, t, c0, c1)
+                    both = window[t][:, c1 : c0 + n].unsqueeze(2).to_broadcast([P, ORDER_COLS, 2])
+                    nc.scalar.copy(pairs[share][:, 1, n - ORDER_COLS :, :], both)
+            round_into_pairs(nc.scalar.copy, t, V_COLS, 1536)
+            round_into_pairs(nc.scalar.copy, t, 1536, A_COLS)
 
         round_dz(nc.scalar.copy, 0, 0, 256)
         round_dz(nc.vector.tensor_copy, 1, 0, 256)
@@ -151,13 +152,12 @@ def tile_attend_gqr_a_pl_kernel(tc, bT, W, dz, offs, joffs, out_0, out_1, out_2)
         quantize_dz(0)
         for v in range(2):
             round_w(nc.vector.tensor_copy, 0, v)
-            round_w(nc.vector.tensor_copy, 1, v)
-            round_w(nc.scalar.copy, 2, v)
-        quantize_w(0)
+            round_w(nc.scalar.copy, 1, v)
+        quantize_w(0, 0, 1)
         product(0)
-        quantize_w(1)
+        quantize_w(0, 1, 1)
         product(1)
-        quantize_w(2)
+        quantize_w(1, 0, 2)
         product(2)
         product(3)
         gather(1)
@@ -195,10 +195,8 @@ def tile_attend_gqr_a_pl_kernel(tc, bT, W, dz, offs, joffs, out_0, out_1, out_2)
                 if s + w == c0 + n:
                     nc.sync.dma_start(words_out[:, s : s + w], y_codes[:, s : s + w].bitcast(I32))
 
-        round_into_pairs(nc.scalar.copy, 3, V_COLS, A_COLS)
         for c0, w in S_WEAVES:
             weave(nc.scalar.copy, U32, c0, w)
-        round_into_pairs(nc.vector.tensor_copy, 2, 0, V_BOTH)
         round_into_pairs(nc.vector.tensor_copy, 3, V_BOTH, V_COLS)
         round_into_pairs(nc.vector.tensor_copy, 3, 0, V_BOTH)
         for c0, w in V_WEAVES[:3]:

@@ -50,10 +50,10 @@ def tile_attend_gqr_a_pl_kernel(tc, bT, W, dz, offs, joffs, out_0, out_1, out_2)
         dz_raw = sb.tile([P, LANES, ITEMS], F32, name="dz_raw")
         b_table = [sb.tile([P, B_COLS], F32, name=f"b_table{t}") for t in range(LANES)]
         nc.sync.dma_start(dz_raw[:], dz_rows)
-        nc.sync.dma_start(b_list[:], joffs)
-        nc.sync.dma_start(b_table[0][:], b_rows[:, 0, :])
         for v in range(2):
             nc.sync.dma_start(w_raw[v][:], w_rows[:, 2 * v : 2 * v + 2, :])
+        nc.sync.dma_start(b_list[:], joffs)
+        nc.sync.dma_start(b_table[0][:], b_rows[:, 0, :])
         nc.sync.dma_start(b_table[1][:], b_rows[:, 1, :])
         nc.sync.dma_start(a_list[:], offs)
         nc.sync.dma_start(b_table[2][:], b_rows[:, 2, :])
@@ -147,7 +147,6 @@ def tile_attend_gqr_a_pl_kernel(tc, bT, W, dz, offs, joffs, out_0, out_1, out_2)
 
         round_dz(nc.scalar.copy, 0, 0, 256)
         round_dz(nc.vector.tensor_copy, 1, 0, 256)
-        gather(0)
         quantize_dz(1)
         quantize_dz(0)
         for v in range(2):
@@ -160,6 +159,7 @@ def tile_attend_gqr_a_pl_kernel(tc, bT, W, dz, offs, joffs, out_0, out_1, out_2)
         quantize_w(1, 0, 2)
         product(2)
         product(3)
+        gather(0)
         gather(1)
         scatter(0)
         scatter(1)

@@ -116,7 +116,10 @@ def tile_attend_gqr_a_pl_kernel(tc, bT, W, dz, offs, joffs, out_0, out_1, out_2)
 
         def gather(t):
             picked[t] = sb.tile([P, ITEMS], F32, name=f"picked{t}", tag=f"slot{t % 2}", align_bytes=64)
-            nc.vector.tensor_copy(picked[t][:], b_table[t][:].indirect(b_list[:]))
+            if t < 2:
+                nc.vector.tensor_copy(picked[t][:], b_table[t][:].indirect(b_list[:]))
+            else:
+                nc.vector.tensor_tensor(picked[t][:], b_table[t][:].indirect(b_list[:]), de[t][:], MULT)
 
         shares = [(c0, 512) for c0 in range(0, A_COLS, 512)]
         pairs = [sb.tile([P, 2, n, 2], BF16, name=f"pairs{k}", align_bytes=64) for k, (c0, n) in enumerate(shares)]
@@ -130,7 +133,10 @@ def tile_attend_gqr_a_pl_kernel(tc, bT, W, dz, offs, joffs, out_0, out_1, out_2)
             move(pairs[share][:, t // 2, c0 - base : c1 - base, t % 2], window[t][:, c0:c1])
 
         def scatter(t):
-            nc.vector.tensor_tensor(window[t][:].indirect(a_list[:]), de[t][:], picked[t][:], MULT)
+            if t < 2:
+                nc.vector.tensor_tensor(window[t][:].indirect(a_list[:]), de[t][:], picked[t][:], MULT)
+            else:
+                nc.vector.tensor_copy(window[t][:].indirect(a_list[:]), picked[t][:])
             nc.sync.dma_start(out_rows[:, t, :], window[t][:])
             if t < 2:
                 round_into_pairs(nc.scalar.copy, t, 0, V_BOTH)

@@ -11,6 +11,7 @@ U8 = mybir.dt.uint8
 E4M3X4 = mybir.dt.float8_e4m3fn_x4
 E5M2X4 = mybir.dt.float8_e5m2_x4
 MULT = mybir.AluOpType.mult
+COPY = mybir.ActivationFunctionType.Copy
 
 P = 128
 LANES = 4
@@ -18,15 +19,13 @@ D, F, ITEMS = 512, 512, 512
 A_COLS, B_COLS = 2048, 1024
 FLOPS = 2 * D * F * ITEMS
 
-V_COLS = 1024
-V_BOTH = 512
+HALF = ITEMS // 2
 STRIP = 512
-W_GROUPS = [(0, 2), (2, 2)]
-ORDER_COLS = 8
-PIECES = [(c0, 256) for c0 in range(0, A_COLS, 256)]
+PIECE = 256
+V_SHARES = [(0, 512), (512, 640)]
+S_SHARES = [(1152, 448), (1600, 448)]
+SHARES = V_SHARES + S_SHARES
 CODE_STORES = [(0, 512), (512, 512), (1024, 512), (1536, 256), (1792, 256)]
-V_WEAVES = [(512, 256), (0, 256), (256, 256), (768, 256)]
-S_WEAVES = [(1024, 256), (1280, 256), (1536, 256), (1792, 256)]
 
 
 def tile_attend_gqr_a_pl_kernel(tc, bT, W, dz, offs, joffs, out_0, out_1, out_2):
@@ -34,6 +33,7 @@ def tile_attend_gqr_a_pl_kernel(tc, bT, W, dz, offs, joffs, out_0, out_1, out_2)
     with ExitStack() as ctx:
         lists = ctx.enter_context(tc.tile_pool(name="lists", bufs=1))
         sb = ctx.enter_context(tc.tile_pool(name="sb", bufs=1))
+        late = ctx.enter_context(tc.tile_pool(name="late", bufs=1))
         psum = ctx.enter_context(tc.psum_pool(name="psum", bufs=1))
 
         a_list = lists.tile([P, ITEMS // 16], U16, name="a_list")
@@ -46,38 +46,43 @@ def tile_attend_gqr_a_pl_kernel(tc, bT, W, dz, offs, joffs, out_0, out_1, out_2)
         words_out = out_1[0].rearrange("p c l -> p (c l)").bitcast(I32)
         scales_out = out_2[0].bitcast(I32)
 
+        pair_at = [8 * c0 for c0, n in SHARES]
+
         w_raw = [sb.tile([P, 2, D], F32, name=f"w_raw{v}") for v in range(2)]
         dz_raw = sb.tile([P, LANES, ITEMS], F32, name="dz_raw")
-        b_table = [sb.tile([P, B_COLS], F32, name=f"b_table{t}") for t in range(LANES)]
+        b_table = [
+            sb.tile([P, B_COLS], F32, name="b_table0", tag="slot0"),
+            sb.tile([P, B_COLS], F32, name="b_table1", tag="slot1"),
+            sb.tile([P, B_COLS], F32, name="b_table2", tag="slot2"),
+            late.tile([P, B_COLS], F32, name="b_table3", offset=pair_at[1] - 2 * B_COLS),
+        ]
         nc.sync.dma_start(dz_raw[:], dz_rows)
         for v in range(2):
             nc.sync.dma_start(w_raw[v][:], w_rows[:, 2 * v : 2 * v + 2, :])
         nc.sync.dma_start(b_list[:], joffs)
         nc.sync.dma_start(b_table[0][:], b_rows[:, 0, :])
-        nc.sync.dma_start(b_table[1][:], b_rows[:, 1, :])
-        nc.sync.dma_start(a_list[:], offs)
         nc.sync.dma_start(b_table[2][:], b_rows[:, 2, :])
+        nc.sync.dma_start(a_list[:], offs)
+        nc.sync.dma_start(b_table[1][:], b_rows[:, 1, :])
         nc.sync.dma_start(b_table[3][:], b_rows[:, 3, :])
 
-        window = [sb.tile([P, A_COLS], F32, name=f"window{u}") for u in range(2)] * 2
-        for u in range(2):
-            nc.vector.memset(window[u][:].bitcast(I32), 0)
+        window = {}
+        for t in range(2):
+            window[t] = sb.tile([P, A_COLS], F32, name=f"window{t}")
+            nc.vector.memset(window[t][:].bitcast(I32), 0)
 
-        w_tags = ["slot1", "w_bf1"]
-        w_bf = [sb.tile([P, n, P, LANES], BF16, name=f"w_bf{g}", tag=w_tags[g], align_bytes=64) for g, (t0, n) in enumerate(W_GROUPS)]
-        w_codes = [sb.tile([P, n * P], U32, name=f"w_codes{g}", align_bytes=64) for g, (t0, n) in enumerate(W_GROUPS)]
-        w_scales = [sb.tile([P, n * P], U8, name=f"w_scales{g}", align_bytes=64) for g, (t0, n) in enumerate(W_GROUPS)]
-        dz_bf = [sb.tile([P, ITEMS // 2, LANES], BF16, name=f"dz_bf{h}", align_bytes=64) for h in range(2)]
+        w_bf = [sb.tile([P, 2, P, LANES], BF16, name=f"w_bf{g}", align_bytes=64) for g in range(2)]
+        w_codes = [sb.tile([P, 2 * P], U32, name=f"w_codes{g}", align_bytes=64) for g in range(2)]
+        w_scales = [sb.tile([P, 2 * P], U8, name=f"w_scales{g}", align_bytes=64) for g in range(2)]
+        dz_bf = [sb.tile([P, HALF, LANES], BF16, name=f"dz_bf{h}", align_bytes=64) for h in range(2)]
         dz_codes = sb.tile([P, ITEMS], U32, name="dz_codes", align_bytes=64)
         dz_scales = sb.tile([P, ITEMS], U8, name="dz_scales", align_bytes=64)
-        picked = {}
-        de = {}
 
-        def round_dz(move, h, i0, n):
-            move(dz_bf[h][:, i0 : i0 + n, :], dz_raw[:, :, h * 256 + i0 : h * 256 + i0 + n].rearrange("p j i -> p i j"))
+        def round_dz(move, h):
+            move(dz_bf[h][:], dz_raw[:, :, h * HALF : (h + 1) * HALF].rearrange("p j i -> p i j"))
 
         def quantize_dz(h):
-            cols = slice(h * 256, (h + 1) * 256)
+            cols = slice(h * HALF, (h + 1) * HALF)
             nc.vector.quantize_mx(
                 out=dz_codes[:, cols].bitcast(E5M2X4),
                 scales=dz_scales[:, cols],
@@ -85,132 +90,136 @@ def tile_attend_gqr_a_pl_kernel(tc, bT, W, dz, offs, joffs, out_0, out_1, out_2)
             )
 
         def round_w(move, g, v):
-            t0, n = W_GROUPS[g]
             move(
                 w_bf[g][:, :, :, 2 * v : 2 * v + 2].rearrange("p t m j -> p m t j"),
-                w_raw[v][:].rearrange("p j (m t) -> p m t j", t=LANES)[:, :, t0 : t0 + n, :],
+                w_raw[v][:].rearrange("p j (m t) -> p m t j", t=LANES)[:, :, 2 * g : 2 * g + 2, :],
             )
 
-        def quantize_w(u, t0, n):
+        def quantize_w(g, t0, n):
             nc.vector.quantize_mx(
-                out=w_codes[u][:, t0 * P : (t0 + n) * P].bitcast(E4M3X4),
-                scales=w_scales[u][:, t0 * P : (t0 + n) * P],
-                in_=w_bf[u][:, t0 : t0 + n].rearrange("p t m j -> p (t m j)"),
+                out=w_codes[g][:, t0 * P : (t0 + n) * P].bitcast(E4M3X4),
+                scales=w_scales[g][:, t0 * P : (t0 + n) * P],
+                in_=w_bf[g][:, t0 : t0 + n].rearrange("p t m j -> p (t m j)"),
             )
+
+        bank = {}
 
         def product(t):
-            bank = psum.tile([P, ITEMS], F32, name=f"bank{t}")
-            g = t // 2
+            bank[t] = psum.tile([P, ITEMS], F32, name=f"bank{t}")
             cols = slice((t % 2) * P, (t % 2 + 1) * P)
             nc.tensor.matmul_mx(
-                out=bank[:],
-                lhsT=w_codes[g][:, cols].bitcast(E4M3X4),
-                lhsT_scale=w_scales[g][:, cols],
+                out=bank[t][:],
+                lhsT=w_codes[t // 2][:, cols].bitcast(E4M3X4),
+                lhsT_scale=w_scales[t // 2][:, cols],
                 rhs=dz_codes[:].bitcast(E5M2X4),
                 rhs_scale=dz_scales[:],
                 start=True,
                 stop=True,
             )
-            de[t] = sb.tile([P, ITEMS], F32, name=f"de{t}")
-            nc.scalar.copy(de[t][:], bank[:])
 
-        def gather(t):
-            picked[t] = sb.tile([P, ITEMS], F32, name=f"picked{t}", tag=f"slot{t % 2}", align_bytes=64)
-            if t < 2:
-                nc.vector.tensor_copy(picked[t][:], b_table[t][:].indirect(b_list[:]))
-            else:
-                nc.vector.tensor_tensor(picked[t][:], b_table[t][:].indirect(b_list[:]), de[t][:], MULT)
-
-        shares = [(c0, 512) for c0 in range(0, A_COLS, 512)]
-        pairs = [sb.tile([P, 2, n, 2], BF16, name=f"pairs{k}", align_bytes=64) for k, (c0, n) in enumerate(shares)]
-
-        def share_of(c):
-            return max(i for i, (s, n) in enumerate(shares) if s <= c)
-
-        def round_into_pairs(move, t, c0, c1):
-            share = share_of(c0)
-            base = shares[share][0]
-            move(pairs[share][:, t // 2, c0 - base : c1 - base, t % 2], window[t][:, c0:c1])
-
-        def scatter(t):
-            if t < 2:
-                nc.vector.tensor_tensor(window[t][:].indirect(a_list[:]), de[t][:], picked[t][:], MULT)
-            else:
-                nc.vector.tensor_copy(window[t][:].indirect(a_list[:]), picked[t][:])
-            nc.sync.dma_start(out_rows[:, t, :], window[t][:])
-            if t < 2:
-                round_into_pairs(nc.scalar.copy, t, 0, V_BOTH)
-                round_into_pairs(nc.scalar.copy, t, V_BOTH, V_COLS)
-            if t == 2:
-                for share in range(2):
-                    c0, n = shares[share]
-                    c1 = c0 + n - ORDER_COLS
-                    round_into_pairs(nc.scalar.copy, t, c0, c1)
-                    both = window[t][:, c1 : c0 + n].unsqueeze(2).to_broadcast([P, ORDER_COLS, 2])
-                    nc.scalar.copy(pairs[share][:, 1, n - ORDER_COLS :, :], both)
-            round_into_pairs(nc.scalar.copy, t, V_COLS, 1536)
-            round_into_pairs(nc.scalar.copy, t, 1536, A_COLS)
-
-        round_dz(nc.scalar.copy, 0, 0, 256)
-        round_dz(nc.vector.tensor_copy, 1, 0, 256)
+        round_dz(nc.scalar.copy, 0)
+        round_dz(nc.vector.tensor_copy, 1)
         quantize_dz(1)
         quantize_dz(0)
         for v in range(2):
             round_w(nc.vector.tensor_copy, 0, v)
             round_w(nc.scalar.copy, 1, v)
-        quantize_w(0, 0, 1)
-        product(0)
         quantize_w(0, 1, 1)
         product(1)
+        quantize_w(0, 0, 1)
+        product(0)
         quantize_w(1, 0, 2)
         product(2)
         product(3)
-        gather(0)
-        gather(1)
-        scatter(0)
-        scatter(1)
-        gather(2)
-        gather(3)
-        scatter(2)
-        scatter(3)
 
-        y_bf = [sb.tile([P, w * LANES], BF16, name=f"y_bf{k}", align_bytes=64) for k, (c0, w) in enumerate(PIECES)]
+        picked = {}
+        da = {}
+
+        def scalar_scatter(t):
+            for h in range(2):
+                offsets = a_list[:, h * HALF // 16 : (h + 1) * HALF // 16]
+                nc.scalar.activation(window[t][:].indirect(offsets), da[t][:, h * HALF : (h + 1) * HALF], COPY)
+            nc.sync.dma_start(out_rows[:, t, :], window[t][:])
+
+        for t in (0, 2):
+            picked[t] = sb.tile([P, ITEMS], F32, name=f"picked{t}")
+            nc.scalar.activation(picked[t][:], b_table[t][:].indirect(b_list[:]), COPY)
+            window[2 + t // 2] = sb.tile([P, A_COLS], F32, name=f"window{2 + t // 2}", tag=f"slot{t}")
+            nc.gpsimd.memset(window[2 + t // 2][:].bitcast(I32), 0)
+
+        de1 = sb.tile([P, ITEMS], F32, name="de1")
+        nc.vector.tensor_copy(de1[:], bank[1][:])
+        da[0] = sb.tile([P, ITEMS], F32, name="da0")
+        nc.vector.tensor_tensor(da[0][:], bank[0][:], picked[0][:], MULT)
+        scalar_scatter(0)
+        da[1] = sb.tile([P, ITEMS], F32, name="da1")
+        nc.vector.tensor_tensor(da[1][:], b_table[1][:].indirect(b_list[:]), de1[:], MULT)
+        da[2] = sb.tile([P, ITEMS], F32, name="da2", tag="slot1")
+        nc.vector.tensor_tensor(da[2][:], bank[2][:], picked[2][:], MULT)
+        nc.vector.tensor_copy(window[1][:].indirect(a_list[:]), da[1][:])
+        nc.sync.dma_start(out_rows[:, 1, :], window[1][:])
+        scalar_scatter(2)
+        picked[3] = late.tile([P, ITEMS], F32, name="picked3", offset=pair_at[3] - 2 * ITEMS)
+        nc.vector.tensor_copy(picked[3][:], b_table[3][:].indirect(b_list[:]))
+        da[3] = sb.tile([P, ITEMS], F32, name="da3")
+        nc.vector.tensor_tensor(da[3][:], bank[3][:], picked[3][:], MULT)
+        scalar_scatter(3)
+
+        pairs = [late.tile([P, 2, n, 2], BF16, name=f"pairs{k}", offset=pair_at[k]) for k, (c0, n) in enumerate(SHARES)]
+
+        def round_into_pairs(move, t, k):
+            c0, n = SHARES[k]
+            move(pairs[k][:, t // 2, :, t % 2], window[t][:, c0 : c0 + n])
+
+        for t in range(2):
+            for k in range(4):
+                round_into_pairs(nc.vector.tensor_copy, t, k)
+        for t in (2, 3):
+            for k in (1, 0):
+                round_into_pairs(nc.vector.tensor_copy, t, k)
+            for k in (2, 3):
+                round_into_pairs(nc.scalar.copy, t, k)
+
+        y_bf = [sb.tile([P, PIECE * LANES], BF16, name=f"y_bf{k}", align_bytes=64) for k in range(A_COLS // PIECE)]
         y_codes = sb.tile([P, A_COLS], U32, name="y_codes", align_bytes=64)
         y_scales = sb.tile([P, STRIP], U8, name="y_scales", align_bytes=64)
 
-        def weave(move, word, c0, w):
-            k = max(i for i, (s, n) in enumerate(PIECES) if s <= c0)
-            y0 = c0 - PIECES[k][0]
-            share = share_of(c0)
-            c0 -= shares[share][0]
-            words = pairs[share][:].rearrange("p u c e -> p u (c e)").bitcast(word)
+        def weave(move, word, k, c0, c1):
+            base = SHARES[k][0]
+            y0 = c0 % PIECE
+            words = pairs[k][:].rearrange("p u c e -> p u (c e)").bitcast(word)
             move(
-                y_bf[k][:].bitcast(word).rearrange("p (c u) -> p c u", u=2)[:, y0 : y0 + w, :],
-                words[:, :, c0 : c0 + w].rearrange("p u c -> p c u"),
+                y_bf[c0 // PIECE][:].bitcast(word).rearrange("p (c u) -> p c u", u=2)[:, y0 : y0 + c1 - c0, :],
+                words[:, :, c0 - base : c1 - base].rearrange("p u c -> p c u"),
             )
 
+        def weave_share(move, word, k):
+            c0, n = SHARES[k]
+            cuts = [c0] + [c for c in range(0, A_COLS, PIECE) if c0 < c < c0 + n] + [c0 + n]
+            for a, b in zip(cuts, cuts[1:]):
+                weave(move, word, k, a, b)
+
         def quantize_y(k):
-            c0, n = PIECES[k]
+            c0 = k * PIECE
             strip, s0 = divmod(c0, STRIP)
             nc.vector.quantize_mx(
-                out=y_codes[:, c0 : c0 + n].bitcast(E4M3X4),
-                scales=y_scales[4 * strip :, s0 : s0 + n],
+                out=y_codes[:, c0 : c0 + PIECE].bitcast(E4M3X4),
+                scales=y_scales[4 * strip :, s0 : s0 + PIECE],
                 in_=y_bf[k][:],
             )
             for s, w in CODE_STORES:
-                if s + w == c0 + n:
+                if s + w == c0 + PIECE:
                     nc.sync.dma_start(words_out[:, s : s + w], y_codes[:, s : s + w].bitcast(I32))
 
-        for c0, w in S_WEAVES:
-            weave(nc.scalar.copy, U32, c0, w)
-        round_into_pairs(nc.vector.tensor_copy, 3, V_BOTH, V_COLS)
-        round_into_pairs(nc.vector.tensor_copy, 3, 0, V_BOTH)
-        for c0, w in V_WEAVES[:3]:
-            weave(nc.vector.tensor_copy, I32, c0, w)
+        for k in (2, 3):
+            weave_share(nc.scalar.copy, U32, k)
+        weave(nc.vector.tensor_copy, I32, 1, 512, 768)
+        weave_share(nc.vector.tensor_copy, I32, 0)
         quantize_y(0)
         quantize_y(1)
-        weave(nc.vector.tensor_copy, I32, *V_WEAVES[3])
-        for k in range(2, len(PIECES)):
+        weave(nc.vector.tensor_copy, I32, 1, 768, 1024)
+        weave(nc.vector.tensor_copy, I32, 1, 1024, 1152)
+        for k in range(2, A_COLS // PIECE):
             quantize_y(k)
         for q in range(4):
             eng = nc.scalar if q % 2 == 0 else nc.sync

@@ -25,7 +25,7 @@ PIECE = 256
 V_SHARES = [(0, 512), (512, 640)]
 S_SHARES = [(1152, 448), (1600, 448)]
 SHARES = V_SHARES + S_SHARES
-CODE_STORES = [(0, 512), (512, 512), (1024, 512), (1536, 256), (1792, 256)]
+CODE_STORES = [(0, 1024), (1024, 768), (1792, 256)]
 
 
 def tile_attend_gqr_a_pl_kernel(tc, bT, W, dz, offs, joffs, out_0, out_1, out_2):

@@ -22,10 +22,10 @@ FLOPS = 2 * D * F * ITEMS
 HALF = ITEMS // 2
 STRIP = 512
 PIECE = 256
-V_SHARES = [(0, 512), (512, 640)]
-S_SHARES = [(1152, 448), (1600, 448)]
-SHARES = V_SHARES + S_SHARES
-CODE_STORES = [(0, 1024), (1024, 768), (1792, 256)]
+SHARES = [(0, 256), (256, 640), (896, 640), (1536, 512)]
+V_WEAVES = 640
+PIECE_ORDER = [0, 1, 2, 6, 7, 3, 4, 5]
+CODE_STORES = {2: (0, 768), 7: (1536, 512), 4: (768, 512), 5: (1280, 256)}
 
 
 def tile_attend_gqr_a_pl_kernel(tc, bT, W, dz, offs, joffs, out_0, out_1, out_2):
@@ -46,15 +46,15 @@ def tile_attend_gqr_a_pl_kernel(tc, bT, W, dz, offs, joffs, out_0, out_1, out_2)
         words_out = out_1[0].rearrange("p c l -> p (c l)").bitcast(I32)
         scales_out = out_2[0].bitcast(I32)
 
-        pair_at = [8 * c0 for c0, n in SHARES]
+        pair_at = [4 * ITEMS + 8 * c0 for c0, n in SHARES]
 
-        w_raw = [sb.tile([P, 2, D], F32, name=f"w_raw{v}") for v in range(2)]
+        w_raw = [sb.tile([P, 2, D], F32, name="w_raw0"), late.tile([P, 2, D], F32, name="w_raw1", offset=4 * HALF)]
         dz_raw = sb.tile([P, LANES, ITEMS], F32, name="dz_raw")
         b_table = [
             sb.tile([P, B_COLS], F32, name="b_table0", tag="slot0"),
-            sb.tile([P, B_COLS], F32, name="b_table1", tag="slot1"),
+            sb.tile([P, B_COLS], F32, name="b_table1"),
             sb.tile([P, B_COLS], F32, name="b_table2", tag="slot2"),
-            late.tile([P, B_COLS], F32, name="b_table3", offset=pair_at[1] - 2 * B_COLS),
+            late.tile([P, B_COLS], F32, name="b_table3", offset=pair_at[3] - 2 * B_COLS),
         ]
         nc.sync.dma_start(dz_raw[:], dz_rows)
         for v in range(2):
@@ -129,8 +129,8 @@ def tile_attend_gqr_a_pl_kernel(tc, bT, W, dz, offs, joffs, out_0, out_1, out_2)
         quantize_w(0, 0, 1)
         product(0)
         quantize_w(1, 0, 2)
-        product(2)
         product(3)
+        product(2)
 
         picked = {}
         da = {}
@@ -141,63 +141,72 @@ def tile_attend_gqr_a_pl_kernel(tc, bT, W, dz, offs, joffs, out_0, out_1, out_2)
                 nc.scalar.activation(window[t][:].indirect(offsets), da[t][:, h * HALF : (h + 1) * HALF], COPY)
             nc.sync.dma_start(out_rows[:, t, :], window[t][:])
 
+        picked[0] = late.tile([P, ITEMS], F32, name="picked0", offset=4 * HALF * 3)
+        picked[2] = sb.tile([P, ITEMS], F32, name="picked2")
         for t in (0, 2):
-            picked[t] = sb.tile([P, ITEMS], F32, name=f"picked{t}")
             nc.scalar.activation(picked[t][:], b_table[t][:].indirect(b_list[:]), COPY)
             window[2 + t // 2] = sb.tile([P, A_COLS], F32, name=f"window{2 + t // 2}", tag=f"slot{t}")
             nc.gpsimd.memset(window[2 + t // 2][:].bitcast(I32), 0)
 
-        de1 = sb.tile([P, ITEMS], F32, name="de1")
-        nc.vector.tensor_copy(de1[:], bank[1][:])
+        def items(h):
+            return slice(h * HALF, (h + 1) * HALF)
+
+        de = {}
+
+        def copy_product(t):
+            for h in range(2):
+                de[t, h] = late.tile([P, HALF], F32, name=f"de{t}_{h}", offset=4 * HALF * (t + h))
+                nc.vector.tensor_copy(de[t, h][:], bank[t][:, items(h)])
+
+        def gather_times_product(t):
+            da[t] = sb.tile([P, ITEMS], F32, name=f"da{t}")
+            for h in range(2):
+                offsets = b_list[:, h * HALF // 16 : (h + 1) * HALF // 16]
+                nc.vector.tensor_tensor(da[t][:, items(h)], b_table[t][:].indirect(offsets), de[t, h][:], MULT)
+
+        copy_product(1)
         da[0] = sb.tile([P, ITEMS], F32, name="da0")
         nc.vector.tensor_tensor(da[0][:], bank[0][:], picked[0][:], MULT)
+        copy_product(3)
         scalar_scatter(0)
-        da[1] = sb.tile([P, ITEMS], F32, name="da1")
-        nc.vector.tensor_tensor(da[1][:], b_table[1][:].indirect(b_list[:]), de1[:], MULT)
-        da[2] = sb.tile([P, ITEMS], F32, name="da2", tag="slot1")
+        gather_times_product(1)
+        da[2] = late.tile([P, ITEMS], F32, name="da2", offset=0)
         nc.vector.tensor_tensor(da[2][:], bank[2][:], picked[2][:], MULT)
         nc.vector.tensor_copy(window[1][:].indirect(a_list[:]), da[1][:])
         nc.sync.dma_start(out_rows[:, 1, :], window[1][:])
         scalar_scatter(2)
-        picked[3] = late.tile([P, ITEMS], F32, name="picked3", offset=pair_at[3] - 2 * ITEMS)
-        nc.vector.tensor_copy(picked[3][:], b_table[3][:].indirect(b_list[:]))
-        da[3] = sb.tile([P, ITEMS], F32, name="da3")
-        nc.vector.tensor_tensor(da[3][:], bank[3][:], picked[3][:], MULT)
+        gather_times_product(3)
         scalar_scatter(3)
 
         pairs = [late.tile([P, 2, n, 2], BF16, name=f"pairs{k}", offset=pair_at[k]) for k, (c0, n) in enumerate(SHARES)]
 
-        def round_into_pairs(move, t, k):
+        def round_into_pairs(move, t, k, parts):
             c0, n = SHARES[k]
-            move(pairs[k][:, t // 2, :, t % 2], window[t][:, c0 : c0 + n])
+            for s in range(0, n, n // parts):
+                move(pairs[k][:, t // 2, s : s + n // parts, t % 2], window[t][:, c0 + s : c0 + s + n // parts])
 
-        for t in range(2):
-            for k in range(4):
-                round_into_pairs(nc.vector.tensor_copy, t, k)
-        for t in (2, 3):
-            for k in (1, 0):
-                round_into_pairs(nc.vector.tensor_copy, t, k)
-            for k in (2, 3):
-                round_into_pairs(nc.scalar.copy, t, k)
+        for t in range(LANES):
+            for k in range(len(SHARES)):
+                if t >= 2 and k == len(SHARES) - 1:
+                    round_into_pairs(nc.scalar.copy, t, k, 2)
+                else:
+                    round_into_pairs(nc.vector.tensor_copy, t, k, 1)
 
         y_bf = [sb.tile([P, PIECE * LANES], BF16, name=f"y_bf{k}", align_bytes=64) for k in range(A_COLS // PIECE)]
         y_codes = sb.tile([P, A_COLS], U32, name="y_codes", align_bytes=64)
         y_scales = sb.tile([P, STRIP], U8, name="y_scales", align_bytes=64)
 
-        def weave(move, word, k, c0, c1):
-            base = SHARES[k][0]
-            y0 = c0 % PIECE
-            words = pairs[k][:].rearrange("p u c e -> p u (c e)").bitcast(word)
-            move(
-                y_bf[c0 // PIECE][:].bitcast(word).rearrange("p (c u) -> p c u", u=2)[:, y0 : y0 + c1 - c0, :],
-                words[:, :, c0 - base : c1 - base].rearrange("p u c -> p c u"),
-            )
-
-        def weave_share(move, word, k):
-            c0, n = SHARES[k]
-            cuts = [c0] + [c for c in range(0, A_COLS, PIECE) if c0 < c < c0 + n] + [c0 + n]
+        def weave(j):
+            c0 = j * PIECE
+            cuts = sorted({c0, c0 + PIECE} | {c for c in [s for s, n in SHARES] + [V_WEAVES] if c0 < c < c0 + PIECE})
             for a, b in zip(cuts, cuts[1:]):
-                weave(move, word, k, a, b)
+                move, word = (nc.vector.tensor_copy, I32) if a < V_WEAVES else (nc.scalar.copy, U32)
+                k = max(i for i, (s, n) in enumerate(SHARES) if s <= a)
+                words = pairs[k][:].rearrange("p u c e -> p u (c e)").bitcast(word)
+                move(
+                    y_bf[j][:].bitcast(word).rearrange("p (c u) -> p c u", u=2)[:, a - c0 : b - c0, :],
+                    words[:, :, a - SHARES[k][0] : b - SHARES[k][0]].rearrange("p u c -> p c u"),
+                )
 
         def quantize_y(k):
             c0 = k * PIECE
@@ -207,20 +216,14 @@ def tile_attend_gqr_a_pl_kernel(tc, bT, W, dz, offs, joffs, out_0, out_1, out_2)
                 scales=y_scales[4 * strip :, s0 : s0 + PIECE],
                 in_=y_bf[k][:],
             )
-            for s, w in CODE_STORES:
-                if s + w == c0 + PIECE:
-                    nc.sync.dma_start(words_out[:, s : s + w], y_codes[:, s : s + w].bitcast(I32))
+            if k in CODE_STORES:
+                s, w = CODE_STORES[k]
+                nc.sync.dma_start(words_out[:, s : s + w], y_codes[:, s : s + w].bitcast(I32))
 
-        for k in (2, 3):
-            weave_share(nc.scalar.copy, U32, k)
-        weave(nc.vector.tensor_copy, I32, 1, 512, 768)
-        weave_share(nc.vector.tensor_copy, I32, 0)
-        quantize_y(0)
-        quantize_y(1)
-        weave(nc.vector.tensor_copy, I32, 1, 768, 1024)
-        weave(nc.vector.tensor_copy, I32, 1, 1024, 1152)
-        for k in range(2, A_COLS // PIECE):
-            quantize_y(k)
+        for j in PIECE_ORDER:
+            weave(j)
+        for j in PIECE_ORDER:
+            quantize_y(j)
         for q in range(4):
             eng = nc.scalar if q % 2 == 0 else nc.sync
             eng.dma_start(

@@ -89,10 +89,11 @@ def tile_attend_gqr_a_pl_kernel(tc, bT, W, dz, offs, joffs, out_0, out_1, out_2)
                 in_=dz_bf[h][:].rearrange("p i j -> p (i j)"),
             )
 
-        def round_w(move, g, v):
+        def round_w(move, v, t0, n):
+            g, s = divmod(t0, 2)
             move(
-                w_bf[g][:, :, :, 2 * v : 2 * v + 2].rearrange("p t m j -> p m t j"),
-                w_raw[v][:].rearrange("p j (m t) -> p m t j", t=LANES)[:, :, 2 * g : 2 * g + 2, :],
+                w_bf[g][:, s : s + n, :, 2 * v : 2 * v + 2].rearrange("p t m j -> p m t j"),
+                w_raw[v][:].rearrange("p j (m t) -> p m t j", t=LANES)[:, :, t0 : t0 + n, :],
             )
 
         def quantize_w(g, t0, n):
@@ -104,33 +105,44 @@ def tile_attend_gqr_a_pl_kernel(tc, bT, W, dz, offs, joffs, out_0, out_1, out_2)
 
         bank = {}
 
-        def product(t):
-            bank[t] = psum.tile([P, ITEMS], F32, name=f"bank{t}")
+        def items(h):
+            return slice(h * HALF, (h + 1) * HALF)
+
+        def product(t, parts):
             cols = slice((t % 2) * P, (t % 2 + 1) * P)
-            nc.tensor.matmul_mx(
-                out=bank[t][:],
-                lhsT=w_codes[t // 2][:, cols].bitcast(E4M3X4),
-                lhsT_scale=w_scales[t // 2][:, cols],
-                rhs=dz_codes[:].bitcast(E5M2X4),
-                rhs_scale=dz_scales[:],
-                start=True,
-                stop=True,
-            )
+            n = ITEMS // parts
+            for s in range(parts):
+                acc = psum.tile([P, n], F32, name=f"bank{t}_{s}")
+                nc.tensor.matmul_mx(
+                    out=acc[:],
+                    lhsT=w_codes[t // 2][:, cols].bitcast(E4M3X4),
+                    lhsT_scale=w_scales[t // 2][:, cols],
+                    rhs=dz_codes[:, s * n : (s + 1) * n].bitcast(E5M2X4),
+                    rhs_scale=dz_scales[:, s * n : (s + 1) * n],
+                    start=True,
+                    stop=True,
+                )
+                bank[t, s] = acc
+
+        def product_half(t, h):
+            return bank[t, h][:] if (t, 1) in bank else bank[t, 0][:, items(h)]
 
         round_dz(nc.scalar.copy, 0)
         round_dz(nc.vector.tensor_copy, 1)
         quantize_dz(1)
         quantize_dz(0)
-        for v in range(2):
-            round_w(nc.vector.tensor_copy, 0, v)
-            round_w(nc.scalar.copy, 1, v)
+        round_w(nc.vector.tensor_copy, 0, 0, 2)
+        round_w(nc.scalar.copy, 0, 2, 2)
+        round_w(nc.vector.tensor_copy, 1, 1, 1)
+        round_w(nc.vector.tensor_copy, 1, 0, 1)
+        round_w(nc.scalar.copy, 1, 2, 2)
         quantize_w(0, 1, 1)
-        product(1)
+        product(1, 2)
         quantize_w(0, 0, 1)
-        product(0)
+        product(0, 2)
         quantize_w(1, 0, 2)
-        product(3)
-        product(2)
+        product(3, 1)
+        product(2, 1)
 
         picked = {}
         da = {}
@@ -141,22 +153,22 @@ def tile_attend_gqr_a_pl_kernel(tc, bT, W, dz, offs, joffs, out_0, out_1, out_2)
                 nc.scalar.activation(window[t][:].indirect(offsets), da[t][:, h * HALF : (h + 1) * HALF], COPY)
             nc.sync.dma_start(out_rows[:, t, :], window[t][:])
 
-        picked[0] = late.tile([P, ITEMS], F32, name="picked0", offset=4 * HALF * 3)
+        picked[0] = [late.tile([P, HALF], F32, name=f"picked0_{h}", offset=4 * HALF * (3 + h)) for h in range(2)]
         picked[2] = sb.tile([P, ITEMS], F32, name="picked2")
+        for h in range(2):
+            offsets = b_list[:, h * HALF // 16 : (h + 1) * HALF // 16]
+            nc.scalar.activation(picked[0][h][:], b_table[0][:].indirect(offsets), COPY)
+        nc.scalar.activation(picked[2][:], b_table[2][:].indirect(b_list[:]), COPY)
         for t in (0, 2):
-            nc.scalar.activation(picked[t][:], b_table[t][:].indirect(b_list[:]), COPY)
             window[2 + t // 2] = sb.tile([P, A_COLS], F32, name=f"window{2 + t // 2}", tag=f"slot{t}")
             nc.gpsimd.memset(window[2 + t // 2][:].bitcast(I32), 0)
-
-        def items(h):
-            return slice(h * HALF, (h + 1) * HALF)
 
         de = {}
 
         def copy_product(t):
             for h in range(2):
                 de[t, h] = late.tile([P, HALF], F32, name=f"de{t}_{h}", offset=4 * HALF * (t + h))
-                nc.vector.tensor_copy(de[t, h][:], bank[t][:, items(h)])
+                nc.vector.tensor_copy(de[t, h][:], product_half(t, h))
 
         def gather_times_product(t):
             da[t] = sb.tile([P, ITEMS], F32, name=f"da{t}")
@@ -166,12 +178,13 @@ def tile_attend_gqr_a_pl_kernel(tc, bT, W, dz, offs, joffs, out_0, out_1, out_2)
 
         copy_product(1)
         da[0] = sb.tile([P, ITEMS], F32, name="da0")
-        nc.vector.tensor_tensor(da[0][:], bank[0][:], picked[0][:], MULT)
+        for h in range(2):
+            nc.vector.tensor_tensor(da[0][:, items(h)], product_half(0, h), picked[0][h][:], MULT)
         copy_product(3)
         scalar_scatter(0)
         gather_times_product(1)
         da[2] = late.tile([P, ITEMS], F32, name="da2", offset=0)
-        nc.vector.tensor_tensor(da[2][:], bank[2][:], picked[2][:], MULT)
+        nc.vector.tensor_tensor(da[2][:], bank[2, 0][:], picked[2][:], MULT)
         nc.vector.tensor_copy(window[1][:].indirect(a_list[:]), da[1][:])
         nc.sync.dma_start(out_rows[:, 1, :], window[1][:])
         scalar_scatter(2)

@@ -24,6 +24,7 @@ STRIP = 512
 PIECE = 256
 SHARES = [(0, 256), (256, 640), (896, 640), (1536, 512)]
 V_WEAVES = 640
+RUN = 4
 PIECE_ORDER = [0, 1, 2, 6, 7, 3, 4, 5]
 CODE_STORES = {2: (0, 768), 7: (1536, 512), 4: (768, 512), 5: (1280, 256)}
 
@@ -79,7 +80,10 @@ def tile_attend_gqr_a_pl_kernel(tc, bT, W, dz, offs, joffs, out_0, out_1, out_2)
         dz_scales = sb.tile([P, ITEMS], U8, name="dz_scales", align_bytes=64)
 
         def round_dz(move, h):
-            move(dz_bf[h][:], dz_raw[:, :, h * HALF : (h + 1) * HALF].rearrange("p j i -> p i j"))
+            move(
+                dz_bf[h][:].rearrange("p (c i) j -> p c j i", i=RUN),
+                dz_raw[:, :, h * HALF : (h + 1) * HALF].rearrange("p j (c i) -> p c j i", i=RUN),
+            )
 
         def quantize_dz(h):
             cols = slice(h * HALF, (h + 1) * HALF)
@@ -217,8 +221,8 @@ def tile_attend_gqr_a_pl_kernel(tc, bT, W, dz, offs, joffs, out_0, out_1, out_2)
                 k = max(i for i, (s, n) in enumerate(SHARES) if s <= a)
                 words = pairs[k][:].rearrange("p u c e -> p u (c e)").bitcast(word)
                 move(
-                    y_bf[j][:].bitcast(word).rearrange("p (c u) -> p c u", u=2)[:, a - c0 : b - c0, :],
-                    words[:, :, a - SHARES[k][0] : b - SHARES[k][0]].rearrange("p u c -> p c u"),
+                    y_bf[j][:].bitcast(word)[:, 2 * (a - c0) : 2 * (b - c0)].rearrange("p (c i u) -> p c u i", u=2, i=RUN),
+                    words[:, :, a - SHARES[k][0] : b - SHARES[k][0]].rearrange("p u (c i) -> p c u i", i=RUN),
                 )
 
         def quantize_y(k):

@@ -11,6 +11,7 @@ U8 = mybir.dt.uint8
 E4M3X4 = mybir.dt.float8_e4m3fn_x4
 E5M2X4 = mybir.dt.float8_e5m2_x4
 MULT = mybir.AluOpType.mult
+ADD = mybir.AluOpType.add
 COPY = mybir.ActivationFunctionType.Copy
 
 P = 128
@@ -20,13 +21,11 @@ A_COLS, B_COLS = 2048, 1024
 FLOPS = 2 * D * F * ITEMS
 
 HALF = ITEMS // 2
-STRIP = 512
-PIECE = 256
-SHARES = [(0, 256), (256, 640), (896, 640), (1536, 512)]
-V_WEAVES = 640
+STRIP = 1024
+PIECES = [(0, 512), (512, 512), (1024, 256), (1280, 256), (1536, 256), (1792, 256)]
 RUN = 4
-PIECE_ORDER = [0, 1, 2, 6, 7, 3, 4, 5]
-CODE_STORES = {2: (0, 768), 7: (1536, 512), 4: (768, 512), 5: (1280, 256)}
+SHARES = [(0, 960), (960, 576), (1536, 512)]
+CODE_STORES = {0: (0, 512), 2: (512, 768), 4: (1280, 512), 5: (1792, 256)}
 
 
 def tile_attend_gqr_a_pl_kernel(tc, bT, W, dz, offs, joffs, out_0, out_1, out_2):
@@ -47,49 +46,53 @@ def tile_attend_gqr_a_pl_kernel(tc, bT, W, dz, offs, joffs, out_0, out_1, out_2)
         words_out = out_1[0].rearrange("p c l -> p (c l)").bitcast(I32)
         scales_out = out_2[0].bitcast(I32)
 
-        pair_at = [4 * ITEMS + 8 * c0 for c0, n in SHARES]
-
-        w_raw = [sb.tile([P, 2, D], F32, name="w_raw0"), late.tile([P, 2, D], F32, name="w_raw1", offset=4 * HALF)]
+        w_raw = [sb.tile([P, 2, D], F32, name=f"w_raw{v}") for v in range(2)]
         dz_raw = sb.tile([P, LANES, ITEMS], F32, name="dz_raw")
-        b_table = [
-            sb.tile([P, B_COLS], F32, name="b_table0", tag="slot0"),
-            sb.tile([P, B_COLS], F32, name="b_table1"),
-            sb.tile([P, B_COLS], F32, name="b_table2", tag="slot2"),
-            late.tile([P, B_COLS], F32, name="b_table3", offset=pair_at[3] - 2 * B_COLS),
-        ]
+        b_table = [sb.tile([P, B_COLS], F32, name=f"b_table{t}") for t in range(LANES)]
         nc.sync.dma_start(dz_raw[:], dz_rows)
         for v in range(2):
             nc.sync.dma_start(w_raw[v][:], w_rows[:, 2 * v : 2 * v + 2, :])
         nc.sync.dma_start(b_list[:], joffs)
         nc.sync.dma_start(b_table[0][:], b_rows[:, 0, :])
-        nc.sync.dma_start(b_table[2][:], b_rows[:, 2, :])
         nc.sync.dma_start(a_list[:], offs)
-        nc.sync.dma_start(b_table[1][:], b_rows[:, 1, :])
-        nc.sync.dma_start(b_table[3][:], b_rows[:, 3, :])
+        for t in (1, 3, 2):
+            nc.sync.dma_start(b_table[t][:], b_rows[:, t, :])
 
         window = {}
         for t in range(2):
             window[t] = sb.tile([P, A_COLS], F32, name=f"window{t}")
             nc.vector.memset(window[t][:].bitcast(I32), 0)
 
-        w_bf = [sb.tile([P, 2, P, LANES], BF16, name=f"w_bf{g}", align_bytes=64) for g in range(2)]
+        window[3] = sb.tile([P, A_COLS], F32, name="window3")
+        nc.gpsimd.memset(window[3][:].bitcast(I32), 0)
+
+        window_bytes = 4 * A_COLS
+        w_bf = [
+            sb.tile([P, 2, P, LANES], BF16, name="w_bf0", align_bytes=64),
+            late.tile([P, 2, P, LANES], BF16, name="w_bf1", align_bytes=64, offset=window_bytes - 512),
+        ]
         w_codes = [sb.tile([P, 2 * P], U32, name=f"w_codes{g}", align_bytes=64) for g in range(2)]
         w_scales = [sb.tile([P, 2 * P], U8, name=f"w_scales{g}", align_bytes=64) for g in range(2)]
         dz_bf = [sb.tile([P, HALF, LANES], BF16, name=f"dz_bf{h}", align_bytes=64) for h in range(2)]
         dz_codes = sb.tile([P, ITEMS], U32, name="dz_codes", align_bytes=64)
         dz_scales = sb.tile([P, ITEMS], U8, name="dz_scales", align_bytes=64)
 
+        def items(h):
+            return slice(h * HALF, (h + 1) * HALF)
+
+        def entries(tile, h):
+            return tile[:, h * HALF // 16 : (h + 1) * HALF // 16]
+
         def round_dz(move, h):
             move(
                 dz_bf[h][:].rearrange("p (c i) j -> p c j i", i=RUN),
-                dz_raw[:, :, h * HALF : (h + 1) * HALF].rearrange("p j (c i) -> p c j i", i=RUN),
+                dz_raw[:, :, items(h)].rearrange("p j (c i) -> p c j i", i=RUN),
             )
 
         def quantize_dz(h):
-            cols = slice(h * HALF, (h + 1) * HALF)
             nc.vector.quantize_mx(
-                out=dz_codes[:, cols].bitcast(E5M2X4),
-                scales=dz_scales[:, cols],
+                out=dz_codes[:, items(h)].bitcast(E5M2X4),
+                scales=dz_scales[:, items(h)],
                 in_=dz_bf[h][:].rearrange("p i j -> p (i j)"),
             )
 
@@ -109,27 +112,18 @@ def tile_attend_gqr_a_pl_kernel(tc, bT, W, dz, offs, joffs, out_0, out_1, out_2)
 
         bank = {}
 
-        def items(h):
-            return slice(h * HALF, (h + 1) * HALF)
-
-        def product(t, parts):
+        def product(t, s, n):
             cols = slice((t % 2) * P, (t % 2 + 1) * P)
-            n = ITEMS // parts
-            for s in range(parts):
-                acc = psum.tile([P, n], F32, name=f"bank{t}_{s}")
-                nc.tensor.matmul_mx(
-                    out=acc[:],
-                    lhsT=w_codes[t // 2][:, cols].bitcast(E4M3X4),
-                    lhsT_scale=w_scales[t // 2][:, cols],
-                    rhs=dz_codes[:, s * n : (s + 1) * n].bitcast(E5M2X4),
-                    rhs_scale=dz_scales[:, s * n : (s + 1) * n],
-                    start=True,
-                    stop=True,
-                )
-                bank[t, s] = acc
-
-        def product_half(t, h):
-            return bank[t, h][:] if (t, 1) in bank else bank[t, 0][:, items(h)]
+            bank[t, s] = psum.tile([P, n], F32, name=f"bank{t}_{s}")
+            nc.tensor.matmul_mx(
+                out=bank[t, s][:],
+                lhsT=w_codes[t // 2][:, cols].bitcast(E4M3X4),
+                lhsT_scale=w_scales[t // 2][:, cols],
+                rhs=dz_codes[:, s * n : (s + 1) * n].bitcast(E5M2X4),
+                rhs_scale=dz_scales[:, s * n : (s + 1) * n],
+                start=True,
+                stop=True,
+            )
 
         round_dz(nc.scalar.copy, 0)
         round_dz(nc.vector.tensor_copy, 1)
@@ -137,113 +131,125 @@ def tile_attend_gqr_a_pl_kernel(tc, bT, W, dz, offs, joffs, out_0, out_1, out_2)
         quantize_dz(0)
         round_w(nc.vector.tensor_copy, 0, 0, 2)
         round_w(nc.scalar.copy, 0, 2, 2)
-        round_w(nc.vector.tensor_copy, 1, 1, 1)
         round_w(nc.vector.tensor_copy, 1, 0, 1)
+        round_w(nc.vector.tensor_copy, 1, 1, 1)
         round_w(nc.scalar.copy, 1, 2, 2)
-        quantize_w(0, 1, 1)
-        product(1, 2)
         quantize_w(0, 0, 1)
-        product(0, 2)
+        product(0, 0, HALF)
+        product(0, 1, HALF)
+        quantize_w(0, 1, 1)
+        product(1, 0, ITEMS)
         quantize_w(1, 0, 2)
-        product(3, 1)
-        product(2, 1)
+        product(3, 0, ITEMS)
+        product(2, 0, ITEMS)
 
-        picked = {}
-        da = {}
+        window[2] = late.tile([P, A_COLS], F32, name="window2", offset=0)
+        nc.gpsimd.memset(window[2][:].bitcast(I32), 0)
 
-        def scalar_scatter(t):
-            for h in range(2):
-                offsets = a_list[:, h * HALF // 16 : (h + 1) * HALF // 16]
-                nc.scalar.activation(window[t][:].indirect(offsets), da[t][:, h * HALF : (h + 1) * HALF], COPY)
+        rows = [sb.tile([P, LANES, n], BF16, name=f"rows{k}") for k, (c0, n) in enumerate(SHARES)]
+
+        def round_lane(move, t, k):
+            c0, n = SHARES[k]
+            move(rows[k][:, t, :], window[t][:, c0 : c0 + n])
+
+        def gpsimd_round(out, in_):
+            nc.gpsimd.tensor_scalar(out, in_, 1.0, 0.0, MULT, ADD)
+
+        def scalar_gather(t, h, tile):
+            nc.scalar.activation(tile[:], b_table[t][:].indirect(entries(b_list, h)), COPY)
+
+        def scalar_scatter(t, h, values):
+            nc.scalar.activation(window[t][:].indirect(entries(a_list, h)), values, COPY)
+            if h == 1:
+                nc.sync.dma_start(out_rows[:, t, :], window[t][:])
+
+        def vector_scatter(t, values):
+            nc.vector.tensor_copy(window[t][:].indirect(a_list[:]), values[:])
             nc.sync.dma_start(out_rows[:, t, :], window[t][:])
 
-        picked[0] = [late.tile([P, HALF], F32, name=f"picked0_{h}", offset=4 * HALF * (3 + h)) for h in range(2)]
-        picked[2] = sb.tile([P, ITEMS], F32, name="picked2")
+        spare = window_bytes + 8 * ITEMS
+        da0 = []
         for h in range(2):
-            offsets = b_list[:, h * HALF // 16 : (h + 1) * HALF // 16]
-            nc.scalar.activation(picked[0][h][:], b_table[0][:].indirect(offsets), COPY)
-        nc.scalar.activation(picked[2][:], b_table[2][:].indirect(b_list[:]), COPY)
-        for t in (0, 2):
-            window[2 + t // 2] = sb.tile([P, A_COLS], F32, name=f"window{2 + t // 2}", tag=f"slot{t}")
-            nc.gpsimd.memset(window[2 + t // 2][:].bitcast(I32), 0)
-
-        de = {}
-
-        def copy_product(t):
-            for h in range(2):
-                de[t, h] = late.tile([P, HALF], F32, name=f"de{t}_{h}", offset=4 * HALF * (t + h))
-                nc.vector.tensor_copy(de[t, h][:], product_half(t, h))
-
-        def gather_times_product(t):
-            da[t] = sb.tile([P, ITEMS], F32, name=f"da{t}")
-            for h in range(2):
-                offsets = b_list[:, h * HALF // 16 : (h + 1) * HALF // 16]
-                nc.vector.tensor_tensor(da[t][:, items(h)], b_table[t][:].indirect(offsets), de[t, h][:], MULT)
-
-        copy_product(1)
-        da[0] = sb.tile([P, ITEMS], F32, name="da0")
+            picked = sb.tile([P, HALF], F32, name=f"picked0_{h}")
+            scalar_gather(0, h, picked)
+            da0.append(late.tile([P, HALF], F32, name=f"da0_{h}", offset=spare + 4 * HALF * (1 + h)))
+            nc.vector.tensor_tensor(da0[h][:], bank[0, h][:], picked[:], MULT)
+        de1_at = [window_bytes, window_bytes + 4 * ITEMS]
+        de1 = [late.tile([P, HALF], F32, name=f"de1_{h}", offset=de1_at[h]) for h in range(2)]
         for h in range(2):
-            nc.vector.tensor_tensor(da[0][:, items(h)], product_half(0, h), picked[0][h][:], MULT)
-        copy_product(3)
-        scalar_scatter(0)
-        gather_times_product(1)
-        da[2] = late.tile([P, ITEMS], F32, name="da2", offset=0)
-        nc.vector.tensor_tensor(da[2][:], bank[2, 0][:], picked[2][:], MULT)
-        nc.vector.tensor_copy(window[1][:].indirect(a_list[:]), da[1][:])
+            nc.vector.tensor_copy(de1[h][:], bank[1, 0][:, items(h)])
+        picked = {1: sb.tile([P, ITEMS], F32, name="picked1")}
+        picked[3] = late.tile([P, ITEMS], F32, name="picked3", offset=spare)
+        picked[2] = late.tile([P, ITEMS], F32, name="picked2", offset=spare + 4 * ITEMS)
+        da = {}
+
+        def whole_gather(t):
+            nc.scalar.activation(picked[t][:], b_table[t][:].indirect(b_list[:]), COPY)
+
+        def multiply(t, at):
+            da[t] = late.tile([P, ITEMS], F32, name=f"da{t}", offset=at)
+            nc.vector.tensor_tensor(da[t][:], bank[t, 0][:], picked[t][:], MULT)
+
+        def fused_scatter(h):
+            nc.vector.tensor_tensor(window[1][:].indirect(entries(a_list, h)), picked[1][:, items(h)], de1[h][:], MULT)
+
+        scalar_scatter(0, 0, da0[0][:])
+        whole_gather(3)
+        scalar_scatter(0, 1, da0[1][:])
+        whole_gather(2)
+        nc.vector.tensor_copy(picked[1][:], b_table[1][:].indirect(b_list[:]))
+        fused_scatter(0)
+        multiply(3, de1_at[0])
+        fused_scatter(1)
         nc.sync.dma_start(out_rows[:, 1, :], window[1][:])
-        scalar_scatter(2)
-        gather_times_product(3)
-        scalar_scatter(3)
-
-        pairs = [late.tile([P, 2, n, 2], BF16, name=f"pairs{k}", offset=pair_at[k]) for k, (c0, n) in enumerate(SHARES)]
-
-        def round_into_pairs(move, t, k, parts):
-            c0, n = SHARES[k]
-            for s in range(0, n, n // parts):
-                move(pairs[k][:, t // 2, s : s + n // parts, t % 2], window[t][:, c0 + s : c0 + s + n // parts])
-
-        for t in range(LANES):
+        multiply(2, de1_at[1])
+        for t in range(2):
             for k in range(len(SHARES)):
-                if t >= 2 and k == len(SHARES) - 1:
-                    round_into_pairs(nc.scalar.copy, t, k, 2)
-                else:
-                    round_into_pairs(nc.vector.tensor_copy, t, k, 1)
+                round_lane(gpsimd_round, t, k)
+        for h in range(2):
+            scalar_scatter(3, h, da[3][:, items(h)])
+        vector_scatter(2, da[2])
 
-        y_bf = [sb.tile([P, PIECE * LANES], BF16, name=f"y_bf{k}", align_bytes=64) for k in range(A_COLS // PIECE)]
+        for k in (1, 2):
+            round_lane(nc.scalar.copy, 3, k)
+        for k in (1, 2, 0):
+            round_lane(nc.vector.tensor_copy, 2, k)
+        round_lane(nc.vector.tensor_copy, 3, 0)
+
+        y_bf = [sb.tile([P, n, LANES], BF16, name=f"y_bf{j}", align_bytes=64) for j, (c0, n) in enumerate(PIECES)]
         y_codes = sb.tile([P, A_COLS], U32, name="y_codes", align_bytes=64)
         y_scales = sb.tile([P, STRIP], U8, name="y_scales", align_bytes=64)
 
-        def weave(j):
-            c0 = j * PIECE
-            cuts = sorted({c0, c0 + PIECE} | {c for c in [s for s, n in SHARES] + [V_WEAVES] if c0 < c < c0 + PIECE})
+        def interleave(j):
+            c0, width = PIECES[j]
+            cuts = sorted({c0, c0 + width} | {s for s, n in SHARES if c0 < s < c0 + width})
             for a, b in zip(cuts, cuts[1:]):
-                move, word = (nc.vector.tensor_copy, I32) if a < V_WEAVES else (nc.scalar.copy, U32)
                 k = max(i for i, (s, n) in enumerate(SHARES) if s <= a)
-                words = pairs[k][:].rearrange("p u c e -> p u (c e)").bitcast(word)
+                move = nc.vector.tensor_copy if k == 0 else nc.scalar.copy
                 move(
-                    y_bf[j][:].bitcast(word)[:, 2 * (a - c0) : 2 * (b - c0)].rearrange("p (c i u) -> p c u i", u=2, i=RUN),
-                    words[:, :, a - SHARES[k][0] : b - SHARES[k][0]].rearrange("p u (c i) -> p c u i", i=RUN),
+                    y_bf[j][:, a - c0 : b - c0, :].rearrange("p (c i) t -> p c t i", i=RUN),
+                    rows[k][:, :, a - SHARES[k][0] : b - SHARES[k][0]].rearrange("p t (c i) -> p c t i", i=RUN),
                 )
 
-        def quantize_y(k):
-            c0 = k * PIECE
+        def quantize_y(j):
+            c0, width = PIECES[j]
             strip, s0 = divmod(c0, STRIP)
             nc.vector.quantize_mx(
-                out=y_codes[:, c0 : c0 + PIECE].bitcast(E4M3X4),
-                scales=y_scales[4 * strip :, s0 : s0 + PIECE],
-                in_=y_bf[k][:],
+                out=y_codes[:, c0 : c0 + width].bitcast(E4M3X4),
+                scales=y_scales[4 * strip :, s0 : s0 + width],
+                in_=y_bf[j][:].rearrange("p c t -> p (c t)"),
             )
-            if k in CODE_STORES:
-                s, w = CODE_STORES[k]
+            if j in CODE_STORES:
+                s, w = CODE_STORES[j]
                 nc.sync.dma_start(words_out[:, s : s + w], y_codes[:, s : s + w].bitcast(I32))
 
-        for j in PIECE_ORDER:
-            weave(j)
-        for j in PIECE_ORDER:
+        for j in range(len(PIECES)):
+            interleave(j)
+        for j in range(len(PIECES)):
             quantize_y(j)
         for q in range(4):
             eng = nc.scalar if q % 2 == 0 else nc.sync
             eng.dma_start(
-                scales_out[4 * q : 4 * q + 4, :].rearrange("r (s c) -> s r c", s=4),
-                y_scales[32 * q : 32 * q + 16, :].bitcast(I32),
+                scales_out[4 * q : 4 * q + 4, :].rearrange("r (s c) -> s r c", s=2),
+                y_scales[32 * q : 32 * q + 8, :].bitcast(I32),
             )

@@ -24,7 +24,7 @@ HALF = ITEMS // 2
 STRIP = 1024
 PIECES = [(0, 512), (512, 512), (1024, 256), (1280, 256), (1536, 256), (1792, 256)]
 RUN = 4
-SHARES = [(0, 960), (960, 576), (1536, 512)]
+SHARES = [(0, 864), (864, 672), (1536, 512)]
 CODE_STORES = {0: (0, 512), 2: (512, 768), 4: (1280, 512), 5: (1792, 256)}
 
 
@@ -48,7 +48,11 @@ def tile_attend_gqr_a_pl_kernel(tc, bT, W, dz, offs, joffs, out_0, out_1, out_2)
 
         w_raw = [sb.tile([P, 2, D], F32, name=f"w_raw{v}") for v in range(2)]
         dz_raw = sb.tile([P, LANES, ITEMS], F32, name="dz_raw")
-        b_table = [sb.tile([P, B_COLS], F32, name=f"b_table{t}") for t in range(LANES)]
+        window_bytes = 4 * A_COLS
+        table_at = {t: window_bytes + 4 * B_COLS * t for t in (1, 2)}
+        b_table = {t: sb.tile([P, B_COLS], F32, name=f"b_table{t}") for t in (0, 3)}
+        for t in (1, 2):
+            b_table[t] = late.tile([P, B_COLS], F32, name=f"b_table{t}", offset=table_at[t])
         nc.sync.dma_start(dz_raw[:], dz_rows)
         for v in range(2):
             nc.sync.dma_start(w_raw[v][:], w_rows[:, 2 * v : 2 * v + 2, :])
@@ -66,7 +70,6 @@ def tile_attend_gqr_a_pl_kernel(tc, bT, W, dz, offs, joffs, out_0, out_1, out_2)
         window[3] = sb.tile([P, A_COLS], F32, name="window3")
         nc.gpsimd.memset(window[3][:].bitcast(I32), 0)
 
-        window_bytes = 4 * A_COLS
         w_bf = [
             sb.tile([P, 2, P, LANES], BF16, name="w_bf0", align_bytes=64),
             late.tile([P, 2, P, LANES], BF16, name="w_bf1", align_bytes=64, offset=window_bytes - 512),
@@ -131,14 +134,15 @@ def tile_attend_gqr_a_pl_kernel(tc, bT, W, dz, offs, joffs, out_0, out_1, out_2)
         quantize_dz(0)
         round_w(nc.vector.tensor_copy, 0, 0, 2)
         round_w(nc.scalar.copy, 0, 2, 2)
-        round_w(nc.vector.tensor_copy, 1, 0, 1)
         round_w(nc.vector.tensor_copy, 1, 1, 1)
+        round_w(nc.vector.tensor_copy, 1, 0, 1)
         round_w(nc.scalar.copy, 1, 2, 2)
+        quantize_w(0, 1, 1)
+        product(1, 0, HALF)
         quantize_w(0, 0, 1)
         product(0, 0, HALF)
         product(0, 1, HALF)
-        quantize_w(0, 1, 1)
-        product(1, 0, ITEMS)
+        product(1, 1, HALF)
         quantize_w(1, 0, 2)
         product(3, 0, ITEMS)
         product(2, 0, ITEMS)
@@ -155,60 +159,61 @@ def tile_attend_gqr_a_pl_kernel(tc, bT, W, dz, offs, joffs, out_0, out_1, out_2)
         def gpsimd_round(out, in_):
             nc.gpsimd.tensor_scalar(out, in_, 1.0, 0.0, MULT, ADD)
 
-        def scalar_gather(t, h, tile):
-            nc.scalar.activation(tile[:], b_table[t][:].indirect(entries(b_list, h)), COPY)
+        def scalar_move(out, in_):
+            nc.scalar.activation(out, in_, COPY)
 
-        def scalar_scatter(t, h, values):
-            nc.scalar.activation(window[t][:].indirect(entries(a_list, h)), values, COPY)
-            if h == 1:
-                nc.sync.dma_start(out_rows[:, t, :], window[t][:])
+        def gather(move, t, h, out):
+            move(out, b_table[t][:].indirect(entries(b_list, h)))
 
-        def vector_scatter(t, values):
-            nc.vector.tensor_copy(window[t][:].indirect(a_list[:]), values[:])
+        def multiply(t, h, out, picked):
+            sums = bank[t, h][:] if (t, 1) in bank else bank[t, 0][:, items(h)]
+            nc.vector.tensor_tensor(out, sums, picked, MULT)
+
+        def scatter(move, t, h, values):
+            move(window[t][:].indirect(entries(a_list, h)), values)
+
+        def store(t):
             nc.sync.dma_start(out_rows[:, t, :], window[t][:])
 
-        spare = window_bytes + 8 * ITEMS
-        da0 = []
+        def halves(name):
+            return [sb.tile([P, HALF], F32, name=f"{name}_{h}") for h in range(2)]
+
+        picked0, picked1, da0 = halves("picked0"), halves("picked1"), halves("da0")
+        picked3 = late.tile([P, ITEMS], F32, name="picked3", offset=table_at[1])
+        picked2 = [late.tile([P, HALF], F32, name=f"picked2_{h}", offset=table_at[1] + 4 * (ITEMS + h * HALF)) for h in range(2)]
+        de1 = late.tile([P, HALF], F32, name="de1", offset=window_bytes)
+        da1 = sb.tile([P, HALF], F32, name="da1")
+        da2 = sb.tile([P, ITEMS], F32, name="da2")
+        da3 = [sb.tile([P, HALF], F32, name="da3_0"), late.tile([P, HALF], F32, name="da3_1", offset=table_at[2])]
+
         for h in range(2):
-            picked = sb.tile([P, HALF], F32, name=f"picked0_{h}")
-            scalar_gather(0, h, picked)
-            da0.append(late.tile([P, HALF], F32, name=f"da0_{h}", offset=spare + 4 * HALF * (1 + h)))
-            nc.vector.tensor_tensor(da0[h][:], bank[0, h][:], picked[:], MULT)
-        de1_at = [window_bytes, window_bytes + 4 * ITEMS]
-        de1 = [late.tile([P, HALF], F32, name=f"de1_{h}", offset=de1_at[h]) for h in range(2)]
+            gather(scalar_move, 0, h, picked0[h][:])
+        multiply(0, 0, da0[0][:], picked0[0][:])
+        nc.vector.tensor_copy(de1[:], bank[1, 0][:])
+        multiply(0, 1, da0[1][:], picked0[1][:])
         for h in range(2):
-            nc.vector.tensor_copy(de1[h][:], bank[1, 0][:, items(h)])
-        picked = {1: sb.tile([P, ITEMS], F32, name="picked1")}
-        picked[3] = late.tile([P, ITEMS], F32, name="picked3", offset=spare)
-        picked[2] = late.tile([P, ITEMS], F32, name="picked2", offset=spare + 4 * ITEMS)
-        da = {}
-
-        def whole_gather(t):
-            nc.scalar.activation(picked[t][:], b_table[t][:].indirect(b_list[:]), COPY)
-
-        def multiply(t, at):
-            da[t] = late.tile([P, ITEMS], F32, name=f"da{t}", offset=at)
-            nc.vector.tensor_tensor(da[t][:], bank[t, 0][:], picked[t][:], MULT)
-
-        def fused_scatter(h):
-            nc.vector.tensor_tensor(window[1][:].indirect(entries(a_list, h)), picked[1][:, items(h)], de1[h][:], MULT)
-
-        scalar_scatter(0, 0, da0[0][:])
-        whole_gather(3)
-        scalar_scatter(0, 1, da0[1][:])
-        whole_gather(2)
-        nc.vector.tensor_copy(picked[1][:], b_table[1][:].indirect(b_list[:]))
-        fused_scatter(0)
-        multiply(3, de1_at[0])
-        fused_scatter(1)
-        nc.sync.dma_start(out_rows[:, 1, :], window[1][:])
-        multiply(2, de1_at[1])
+            gather(nc.vector.tensor_copy, 1, h, picked1[h][:])
+        scatter(scalar_move, 0, 0, da0[0][:])
+        scatter(scalar_move, 0, 1, da0[1][:])
+        store(0)
+        scalar_move(picked3[:], b_table[3][:].indirect(b_list[:]))
+        nc.vector.tensor_tensor(window[1][:].indirect(entries(a_list, 0)), picked1[0][:], de1[:], MULT)
+        multiply(1, 1, da1[:], picked1[1][:])
+        scatter(nc.vector.tensor_copy, 1, 1, da1[:])
+        store(1)
+        multiply(3, 0, da3[0][:], picked3[:, items(0)])
         for t in range(2):
             for k in range(len(SHARES)):
                 round_lane(gpsimd_round, t, k)
         for h in range(2):
-            scalar_scatter(3, h, da[3][:, items(h)])
-        vector_scatter(2, da[2])
+            gather(scalar_move, 2, h, picked2[h][:])
+            multiply(2, h, da2[:, items(h)], picked2[h][:])
+        multiply(3, 1, da3[1][:], picked3[:, items(1)])
+        nc.vector.tensor_copy(window[2][:].indirect(a_list[:]), da2[:])
+        for h in range(2):
+            scatter(scalar_move, 3, h, da3[h][:])
+        store(3)
+        store(2)
 
         for k in (1, 2):
             round_lane(nc.scalar.copy, 3, k)

@@ -24,8 +24,9 @@ HALF = ITEMS // 2
 STRIP = 1024
 PIECES = [(0, 512), (512, 512), (1024, 256), (1280, 256), (1536, 256), (1792, 256)]
 RUN = 4
-SHARES = [(0, 864), (864, 672), (1536, 512)]
-CODE_STORES = {0: (0, 512), 2: (512, 768), 4: (1280, 512), 5: (1792, 256)}
+SHARES = [(0, 896), (896, 384), (1280, 768)]
+G_ROUNDS = 512
+CODE_STORES = {0: (0, 512), 1: (512, 512), 3: (1024, 512), 5: (1536, 512)}
 
 
 def tile_attend_gqr_a_pl_kernel(tc, bT, W, dz, offs, joffs, out_0, out_1, out_2):
@@ -152,9 +153,9 @@ def tile_attend_gqr_a_pl_kernel(tc, bT, W, dz, offs, joffs, out_0, out_1, out_2)
 
         rows = [sb.tile([P, LANES, n], BF16, name=f"rows{k}") for k, (c0, n) in enumerate(SHARES)]
 
-        def round_lane(move, t, k):
+        def round_lane(move, t, k, a=0, b=None):
             c0, n = SHARES[k]
-            move(rows[k][:, t, :], window[t][:, c0 : c0 + n])
+            move(rows[k][:, t, a : b or n], window[t][:, c0 + a : c0 + (b or n)])
 
         def gpsimd_round(out, in_):
             nc.gpsimd.tensor_scalar(out, in_, 1.0, 0.0, MULT, ADD)
@@ -219,7 +220,8 @@ def tile_attend_gqr_a_pl_kernel(tc, bT, W, dz, offs, joffs, out_0, out_1, out_2)
             round_lane(nc.scalar.copy, 3, k)
         for k in (1, 2, 0):
             round_lane(nc.vector.tensor_copy, 2, k)
-        round_lane(nc.vector.tensor_copy, 3, 0)
+        round_lane(gpsimd_round, 3, 0, 0, G_ROUNDS)
+        round_lane(nc.vector.tensor_copy, 3, 0, G_ROUNDS)
 
         y_bf = [sb.tile([P, n, LANES], BF16, name=f"y_bf{j}", align_bytes=64) for j, (c0, n) in enumerate(PIECES)]
         y_codes = sb.tile([P, A_COLS], U32, name="y_codes", align_bytes=64)

@@ -21,12 +21,13 @@ A_COLS, B_COLS = 2048, 1024
 FLOPS = 2 * D * F * ITEMS
 
 HALF = ITEMS // 2
-STRIP = 1024
+STRIP = 512
+CALL = 256
 PIECES = [(0, 512), (512, 512), (1024, 256), (1280, 256), (1536, 256), (1792, 256)]
 RUN = 4
 SHARES = [(0, 896), (896, 384), (1280, 768)]
 G_ROUNDS = 512
-CODE_STORES = {0: (0, 512), 1: (512, 512), 3: (1024, 512), 5: (1536, 512)}
+CODE_STORES = {1: (0, 512), 3: (512, 512), 5: (1024, 512), 7: (1536, 512)}
 
 
 def tile_attend_gqr_a_pl_kernel(tc, bT, W, dz, offs, joffs, out_0, out_1, out_2):
@@ -239,12 +240,14 @@ def tile_attend_gqr_a_pl_kernel(tc, bT, W, dz, offs, joffs, out_0, out_1, out_2)
                 )
 
         def quantize_y(j):
-            c0, width = PIECES[j]
+            c0 = j * CALL
+            k = max(i for i, (s, n) in enumerate(PIECES) if s <= c0)
+            at = c0 - PIECES[k][0]
             strip, s0 = divmod(c0, STRIP)
             nc.vector.quantize_mx(
-                out=y_codes[:, c0 : c0 + width].bitcast(E4M3X4),
-                scales=y_scales[4 * strip :, s0 : s0 + width],
-                in_=y_bf[j][:].rearrange("p c t -> p (c t)"),
+                out=y_codes[:, c0 : c0 + CALL].bitcast(E4M3X4),
+                scales=y_scales[4 * strip :, s0 : s0 + CALL],
+                in_=y_bf[k][:, at : at + CALL, :].rearrange("p c t -> p (c t)"),
             )
             if j in CODE_STORES:
                 s, w = CODE_STORES[j]
@@ -252,11 +255,11 @@ def tile_attend_gqr_a_pl_kernel(tc, bT, W, dz, offs, joffs, out_0, out_1, out_2)
 
         for j in range(len(PIECES)):
             interleave(j)
-        for j in range(len(PIECES)):
+        for j in range(A_COLS // CALL):
             quantize_y(j)
         for q in range(4):
             eng = nc.scalar if q % 2 == 0 else nc.sync
             eng.dma_start(
-                scales_out[4 * q : 4 * q + 4, :].rearrange("r (s c) -> s r c", s=2),
-                y_scales[32 * q : 32 * q + 8, :].bitcast(I32),
+                scales_out[4 * q : 4 * q + 4, :].rearrange("r (s c) -> s r c", s=4),
+                y_scales[32 * q : 32 * q + 16, :].bitcast(I32),
             )

@@ -27,7 +27,7 @@ PIECES = [(0, 512), (512, 512), (1024, 256), (1280, 256), (1536, 256), (1792, 25
 RUN = 4
 SHARES = [(0, 896), (896, 384), (1280, 768)]
 G_ROUNDS = 512
-CODE_STORES = {1: (0, 512), 3: (512, 512), 5: (1024, 512), 7: (1536, 512)}
+CODE_STORES = {1: (0, 512), 3: (512, 512), 5: (1024, 512), 6: (1536, 256), 7: (1792, 256)}
 
 
 def tile_attend_gqr_a_pl_kernel(tc, bT, W, dz, offs, joffs, out_0, out_1, out_2):

from contextlib import ExitStack

import concourse.mybir as mybir

F32 = mybir.dt.float32
BF16 = mybir.dt.bfloat16
I32 = mybir.dt.int32
U32 = mybir.dt.uint32
U16 = mybir.dt.uint16
U8 = mybir.dt.uint8
E4M3X4 = mybir.dt.float8_e4m3fn_x4
E5M2X4 = mybir.dt.float8_e5m2_x4
MULT = mybir.AluOpType.mult
ADD = mybir.AluOpType.add
COPY = mybir.ActivationFunctionType.Copy

P = 128
LANES = 4
D, F, ITEMS = 512, 512, 512
A_COLS, B_COLS = 2048, 1024
FLOPS = 2 * D * F * ITEMS

HALF = ITEMS // 2
STRIP = 512
CALL = 256
PIECES = [(0, 512), (512, 512), (1024, 256), (1280, 256), (1536, 256), (1792, 256)]
RUN = 4
SHARES = [(0, 896), (896, 384), (1280, 768)]
G_ROUNDS = 512
CODE_STORES = {1: (0, 512), 3: (512, 512), 5: (1024, 512), 6: (1536, 256), 7: (1792, 256)}


def tile_attend_gqr_a_pl_kernel(tc, bT, W, dz, offs, joffs, out_0, out_1, out_2):
    nc = tc.nc
    with ExitStack() as ctx:
        lists = ctx.enter_context(tc.tile_pool(name="lists", bufs=1))
        sb = ctx.enter_context(tc.tile_pool(name="sb", bufs=1))
        late = ctx.enter_context(tc.tile_pool(name="late", bufs=1))
        psum = ctx.enter_context(tc.psum_pool(name="psum", bufs=1))

        a_list = lists.tile([P, ITEMS // 16], U16, name="a_list")
        b_list = lists.tile([P, ITEMS // 16], U16, name="b_list")

        w_rows = W.rearrange("(p j) d -> p j d", j=LANES)
        dz_rows = dz.rearrange("(p j) i -> p j i", j=LANES)
        b_rows = bT.rearrange("(p t) c -> p t c", t=LANES)
        out_rows = out_0.rearrange("(p t) c -> p t c", t=LANES)
        words_out = out_1[0].rearrange("p c l -> p (c l)").bitcast(I32)
        scales_out = out_2[0].bitcast(I32)

        w_raw = [sb.tile([P, 2, D], F32, name=f"w_raw{v}") for v in range(2)]
        dz_raw = sb.tile([P, LANES, ITEMS], F32, name="dz_raw")
        window_bytes = 4 * A_COLS
        table_at = {t: window_bytes + 4 * B_COLS * t for t in (1, 2)}
        b_table = {t: sb.tile([P, B_COLS], F32, name=f"b_table{t}") for t in (0, 3)}
        for t in (1, 2):
            b_table[t] = late.tile([P, B_COLS], F32, name=f"b_table{t}", offset=table_at[t])
        nc.sync.dma_start(dz_raw[:], dz_rows)
        for v in range(2):
            nc.sync.dma_start(w_raw[v][:], w_rows[:, 2 * v : 2 * v + 2, :])
        nc.sync.dma_start(b_list[:], joffs)
        nc.sync.dma_start(b_table[0][:], b_rows[:, 0, :])
        nc.sync.dma_start(a_list[:], offs)
        for t in (1, 3, 2):
            nc.sync.dma_start(b_table[t][:], b_rows[:, t, :])

        window = {}
        for t in range(2):
            window[t] = sb.tile([P, A_COLS], F32, name=f"window{t}")
            nc.vector.memset(window[t][:].bitcast(I32), 0)

        window[3] = sb.tile([P, A_COLS], F32, name="window3")
        nc.gpsimd.memset(window[3][:].bitcast(I32), 0)

        w_bf = [
            sb.tile([P, 2, P, LANES], BF16, name="w_bf0", align_bytes=64),
            late.tile([P, 2, P, LANES], BF16, name="w_bf1", align_bytes=64, offset=window_bytes - 512),
        ]
        w_codes = [sb.tile([P, 2 * P], U32, name=f"w_codes{g}", align_bytes=64) for g in range(2)]
        w_scales = [sb.tile([P, 2 * P], U8, name=f"w_scales{g}", align_bytes=64) for g in range(2)]
        dz_bf = [sb.tile([P, HALF, LANES], BF16, name=f"dz_bf{h}", align_bytes=64) for h in range(2)]
        dz_codes = sb.tile([P, ITEMS], U32, name="dz_codes", align_bytes=64)
        dz_scales = sb.tile([P, ITEMS], U8, name="dz_scales", align_bytes=64)

        def items(h):
            return slice(h * HALF, (h + 1) * HALF)

        def entries(tile, h):
            return tile[:, h * HALF // 16 : (h + 1) * HALF // 16]

        def round_dz(move, h):
            move(
                dz_bf[h][:].rearrange("p (c i) j -> p c j i", i=RUN),
                dz_raw[:, :, items(h)].rearrange("p j (c i) -> p c j i", i=RUN),
            )

        def quantize_dz(h):
            nc.vector.quantize_mx(
                out=dz_codes[:, items(h)].bitcast(E5M2X4),
                scales=dz_scales[:, items(h)],
                in_=dz_bf[h][:].rearrange("p i j -> p (i j)"),
            )

        def round_w(move, v, t0, n):
            g, s = divmod(t0, 2)
            move(
                w_bf[g][:, s : s + n, :, 2 * v : 2 * v + 2].rearrange("p t m j -> p m t j"),
                w_raw[v][:].rearrange("p j (m t) -> p m t j", t=LANES)[:, :, t0 : t0 + n, :],
            )

        def quantize_w(g, t0, n):
            nc.vector.quantize_mx(
                out=w_codes[g][:, t0 * P : (t0 + n) * P].bitcast(E4M3X4),
                scales=w_scales[g][:, t0 * P : (t0 + n) * P],
                in_=w_bf[g][:, t0 : t0 + n].rearrange("p t m j -> p (t m j)"),
            )

        bank = {}

        def product(t, s, n):
            cols = slice((t % 2) * P, (t % 2 + 1) * P)
            bank[t, s] = psum.tile([P, n], F32, name=f"bank{t}_{s}")
            nc.tensor.matmul_mx(
                out=bank[t, s][:],
                lhsT=w_codes[t // 2][:, cols].bitcast(E4M3X4),
                lhsT_scale=w_scales[t // 2][:, cols],
                rhs=dz_codes[:, s * n : (s + 1) * n].bitcast(E5M2X4),
                rhs_scale=dz_scales[:, s * n : (s + 1) * n],
                start=True,
                stop=True,
            )

        round_dz(nc.scalar.copy, 0)
        round_dz(nc.vector.tensor_copy, 1)
        quantize_dz(1)
        quantize_dz(0)
        round_w(nc.vector.tensor_copy, 0, 0, 2)
        round_w(nc.scalar.copy, 0, 2, 2)
        round_w(nc.vector.tensor_copy, 1, 1, 1)
        round_w(nc.vector.tensor_copy, 1, 0, 1)
        round_w(nc.scalar.copy, 1, 2, 2)
        quantize_w(0, 1, 1)
        product(1, 0, HALF)
        quantize_w(0, 0, 1)
        product(0, 0, HALF)
        product(0, 1, HALF)
        product(1, 1, HALF)
        quantize_w(1, 0, 2)
        product(3, 0, ITEMS)
        product(2, 0, ITEMS)

        window[2] = late.tile([P, A_COLS], F32, name="window2", offset=0)
        nc.gpsimd.memset(window[2][:].bitcast(I32), 0)

        rows = [sb.tile([P, LANES, n], BF16, name=f"rows{k}") for k, (c0, n) in enumerate(SHARES)]

        def round_lane(move, t, k, a=0, b=None):
            c0, n = SHARES[k]
            move(rows[k][:, t, a : b or n], window[t][:, c0 + a : c0 + (b or n)])

        def gpsimd_round(out, in_):
            nc.gpsimd.tensor_scalar(out, in_, 1.0, 0.0, MULT, ADD)

        def scalar_move(out, in_):
            nc.scalar.activation(out, in_, COPY)

        def gather(move, t, h, out):
            move(out, b_table[t][:].indirect(entries(b_list, h)))

        def multiply(t, h, out, picked):
            sums = bank[t, h][:] if (t, 1) in bank else bank[t, 0][:, items(h)]
            nc.vector.tensor_tensor(out, sums, picked, MULT)

        def scatter(move, t, h, values):
            move(window[t][:].indirect(entries(a_list, h)), values)

        def store(t):
            nc.sync.dma_start(out_rows[:, t, :], window[t][:])

        def halves(name):
            return [sb.tile([P, HALF], F32, name=f"{name}_{h}") for h in range(2)]

        picked0, picked1, da0 = halves("picked0"), halves("picked1"), halves("da0")
        picked3 = late.tile([P, ITEMS], F32, name="picked3", offset=table_at[1])
        picked2 = [late.tile([P, HALF], F32, name=f"picked2_{h}", offset=table_at[1] + 4 * (ITEMS + h * HALF)) for h in range(2)]
        de1 = late.tile([P, HALF], F32, name="de1", offset=window_bytes)
        da1 = sb.tile([P, HALF], F32, name="da1")
        da2 = sb.tile([P, ITEMS], F32, name="da2")
        da3 = [sb.tile([P, HALF], F32, name="da3_0"), late.tile([P, HALF], F32, name="da3_1", offset=table_at[2])]

        for h in range(2):
            gather(scalar_move, 0, h, picked0[h][:])
        multiply(0, 0, da0[0][:], picked0[0][:])
        nc.vector.tensor_copy(de1[:], bank[1, 0][:])
        multiply(0, 1, da0[1][:], picked0[1][:])
        for h in range(2):
            gather(nc.vector.tensor_copy, 1, h, picked1[h][:])
        scatter(scalar_move, 0, 0, da0[0][:])
        scatter(scalar_move, 0, 1, da0[1][:])
        store(0)
        scalar_move(picked3[:], b_table[3][:].indirect(b_list[:]))
        nc.vector.tensor_tensor(window[1][:].indirect(entries(a_list, 0)), picked1[0][:], de1[:], MULT)
        multiply(1, 1, da1[:], picked1[1][:])
        scatter(nc.vector.tensor_copy, 1, 1, da1[:])
        store(1)
        multiply(3, 0, da3[0][:], picked3[:, items(0)])
        for t in range(2):
            for k in range(len(SHARES)):
                round_lane(gpsimd_round, t, k)
        for h in range(2):
            gather(scalar_move, 2, h, picked2[h][:])
            multiply(2, h, da2[:, items(h)], picked2[h][:])
        multiply(3, 1, da3[1][:], picked3[:, items(1)])
        nc.vector.tensor_copy(window[2][:].indirect(a_list[:]), da2[:])
        for h in range(2):
            scatter(scalar_move, 3, h, da3[h][:])
        store(3)
        store(2)

        for k in (1, 2):
            round_lane(nc.scalar.copy, 3, k)
        for k in (1, 2, 0):
            round_lane(nc.vector.tensor_copy, 2, k)
        round_lane(gpsimd_round, 3, 0, 0, G_ROUNDS)
        round_lane(nc.vector.tensor_copy, 3, 0, G_ROUNDS)

        y_bf = [sb.tile([P, n, LANES], BF16, name=f"y_bf{j}", align_bytes=64) for j, (c0, n) in enumerate(PIECES)]
        y_codes = sb.tile([P, A_COLS], U32, name="y_codes", align_bytes=64)
        y_scales = sb.tile([P, STRIP], U8, name="y_scales", align_bytes=64)

        def interleave(j):
            c0, width = PIECES[j]
            cuts = sorted({c0, c0 + width} | {s for s, n in SHARES if c0 < s < c0 + width})
            for a, b in zip(cuts, cuts[1:]):
                k = max(i for i, (s, n) in enumerate(SHARES) if s <= a)
                move = nc.vector.tensor_copy if k == 0 else nc.scalar.copy
                move(
                    y_bf[j][:, a - c0 : b - c0, :].rearrange("p (c i) t -> p c t i", i=RUN),
                    rows[k][:, :, a - SHARES[k][0] : b - SHARES[k][0]].rearrange("p t (c i) -> p c t i", i=RUN),
                )

        def quantize_y(j):
            c0 = j * CALL
            k = max(i for i, (s, n) in enumerate(PIECES) if s <= c0)
            at = c0 - PIECES[k][0]
            strip, s0 = divmod(c0, STRIP)
            nc.vector.quantize_mx(
                out=y_codes[:, c0 : c0 + CALL].bitcast(E4M3X4),
                scales=y_scales[4 * strip :, s0 : s0 + CALL],
                in_=y_bf[k][:, at : at + CALL, :].rearrange("p c t -> p (c t)"),
            )
            if j in CODE_STORES:
                s, w = CODE_STORES[j]
                nc.sync.dma_start(words_out[:, s : s + w], y_codes[:, s : s + w].bitcast(I32))

        for j in range(len(PIECES)):
            interleave(j)
        for j in range(A_COLS // CALL):
            quantize_y(j)
        for q in range(4):
            eng = nc.scalar if q % 2 == 0 else nc.sync
            eng.dma_start(
                scales_out[4 * q : 4 * q + 4, :].rearrange("r (s c) -> s r c", s=4),
                y_scales[32 * q : 32 * q + 16, :].bitcast(I32),
            )
